import numpy as np
import ml_dtypes


def mxq(x, axis, fmt="e4m3"):
    dtype, down = {"e4m3": (ml_dtypes.float8_e4m3fn, 7), "e5m2": (ml_dtypes.float8_e5m2, 14)}[fmt]
    v = np.moveaxis(np.asarray(x, np.float32).astype(ml_dtypes.bfloat16).astype(np.float64), axis, -1)
    blocks = v.reshape(v.shape[:-1] + (-1, 32))
    amax = np.abs(blocks).max(-1, keepdims=True)
    byte = np.maximum(np.where(amax > 0, np.frexp(amax)[1] - 1 + 127, 0) - down, 1)
    scale = np.exp2(byte - 127.0)
    codes = (blocks / scale).astype(np.float32).astype(dtype).astype(np.float64)
    return np.moveaxis((codes * scale).reshape(v.shape), -1, axis)


WIDE = False


def mx_kscale(k):
    if not WIDE:
        return np.ones(k)
    levels = np.array([10, -10, 5, -5, 0])
    if k % 512:
        return np.exp2(np.random.permutation(np.resize(levels, k // 32))).repeat(32)
    a = np.empty((k // 512, 16))
    for p in range(k // 512):
        a[p, :8] = np.random.permutation(np.resize(levels, 8))
        for g in range(8):
            far = levels[np.abs(levels - a[p, g]) >= 10]
            a[p, g + 8] = far[np.random.randint(len(far))]
    return np.exp2(a.ravel()).repeat(32)


def f64(x):
    return np.asarray(x).astype(np.float64)


def striped(idx):
    return np.tile(idx.reshape(-1, 16).T, (8, 1)).astype(np.uint16)


def unstriped(offs):
    return offs[:16].T.reshape(-1).astype(np.int64)


def pack_weight(w):
    k, n = w.shape
    w = f64(np.asarray(w, np.float32).astype(ml_dtypes.bfloat16)).reshape(k // 32, 32, n)
    amax = np.abs(w).max(1)
    byte = np.clip(np.where(amax > 0, np.frexp(amax)[1] - 1 + 127 - 7, 1), 1, 254)
    scaled = (w * np.exp2(127.0 - byte)[:, None, :]).reshape(k, n).astype(np.float32)
    words = np.ascontiguousarray(scaled.reshape(k // 512, 128, 4, n).transpose(0, 1, 3, 2)).astype(ml_dtypes.float8_e4m3fn).view(np.uint8)
    return words, np.ascontiguousarray(byte.astype(np.uint8).reshape(k // 512, 16, n))


def unpack_weight(words, scales):
    g, p, n, _ = words.shape
    vals = np.ascontiguousarray(words).view(ml_dtypes.float8_e4m3fn).astype(np.float64) * np.repeat(np.exp2(scales.astype(np.float64) - 127.0), 8, axis=1)[..., None]
    return vals.transpose(0, 1, 3, 2).reshape(g * 512, n)


E2M1 = np.array([0.0, 0.5, 1.0, 1.5, 2.0, 3.0, 4.0, 6.0, -0.0, -0.5, -1.0, -1.5, -2.0, -3.0, -4.0, -6.0])


def pack_fp4(w):
    k, n = w.shape
    w = f64(np.asarray(w, np.float32).astype(ml_dtypes.bfloat16)).reshape(k // 32, 32, n)
    amax = np.abs(w).max(1)
    mant, ex = np.frexp(amax / 6.0)
    byte = np.clip(np.where(amax > 0, np.where(mant > 0.5, ex, ex - 1) + 127, 1), 1, 254)
    scaled = (w * np.exp2(127.0 - byte)[:, None, :]).reshape(k, n).astype(np.float32)
    c = np.ascontiguousarray(scaled.reshape(k // 512, 128, 4, n).transpose(0, 1, 3, 2)).astype(ml_dtypes.float4_e2m1fn).view(np.uint8) & 0xF
    words = (c[..., 0::2] | (c[..., 1::2] << 4)).reshape(k // 512, 128, 2 * n)
    return np.ascontiguousarray(words), np.ascontiguousarray(byte.astype(np.uint8).reshape(k // 512, 16, n))


def unpack_fp4(words, scales):
    g, _, n = scales.shape
    words = np.ascontiguousarray(words).reshape(g, 128, n, 2)
    nib = np.empty((g, 128, n, 4), np.uint8)
    nib[..., 0::2] = words & 0xF
    nib[..., 1::2] = words >> 4
    vals = E2M1[nib] * np.repeat(np.exp2(scales.astype(np.float64) - 127.0), 8, axis=1)[..., None]
    return vals.transpose(0, 1, 3, 2).reshape(g * 512, n)


K, T, S, D, N, H, V, U = 1024, 4096, 1024, 4, 256, 512, 256, 512


def setup_inputs():
    n = np.random.standard_normal
    s = mx_kscale(K)[:, None]
    u = mx_kscale(H)
    packed_xT = pack_weight(n((K, T)) * s)
    packed_w1 = pack_fp4(n((K, H)) / np.sqrt(K) / s)
    packed_w2 = pack_fp4(n((K, H)) / np.sqrt(K) / s)
    packed_w3 = pack_fp4(n((H, N)) / np.sqrt(H) / u[:, None])
    return {
        "x_words": packed_xT[0],
        "x_scales": packed_xT[1],
        "w1_words": packed_w1[0],
        "w1_scales": packed_w1[1],
        "w2_words": packed_w2[0],
        "w2_scales": packed_w2[1],
        "sel": (np.random.uniform(0.1, 0.9, (H, U))).astype(np.float32),
        "unit": (np.random.uniform(0.6, 1.4, (H, 1)) * u[:, None]).astype(np.float32),
        "w3_words": packed_w3[0],
        "w3_scales": packed_w3[1],
        "offs": striped(np.random.permutation(T)[:S]),
        "jn": striped(np.random.permutation(S)),
        "qry": striped(np.random.permutation(np.concatenate([np.arange(V), np.random.randint(0, V, U - V)]))),
    }


def reference(x_words, x_scales, w1_words, w1_scales, w2_words, w2_scales, sel, unit, w3_words, w3_scales, offs, jn, qry):
    xq = unpack_weight(x_words, x_scales)[:, unstriped(offs)]
    cf = unpack_fp4(w1_words, w1_scales).T @ xq
    freq = np.log(np.exp(cf) + 1.0)
    cg = unpack_fp4(w2_words, w2_scales).T @ xq
    frq2 = np.log(np.exp(cg) + 1.0)
    gj = frq2[:, unstriped(jn)]
    match = freq * gj
    size = match.reshape(len(match), -1, D).sum(axis=2)
    sq2 = size[:, unstriped(qry)]
    est = sq2 * f64(sel) + 1.0
    heavy = freq.reshape(len(freq), -1, D).max(axis=2)
    mq = heavy[:, unstriped(qry)]
    hid = f64(unit) * (est / (mq + 0.5))
    return unpack_fp4(w3_words, w3_scales).T @ mxq(hid, 0, "e4m3")

@@ -1,0 +1,300 @@
+from contextlib import ExitStack
+
+import concourse.mybir as mybir
+
+K, T, S, D, N, H, V, U = 1024, 4096, 1024, 4, 256, 512, 256, 512
+FLOPS = 2 * (2 * K * H * S + H * N * U)
+
+F32 = mybir.dt.float32
+BF16 = mybir.dt.bfloat16
+I32 = mybir.dt.int32
+U32 = mybir.dt.uint32
+U16 = mybir.dt.uint16
+U8 = mybir.dt.uint8
+FP8X4 = mybir.dt.float8_e4m3fn_x4
+FP4X4 = mybir.dt.float4_e2m1fn_x4
+ACT = mybir.ActivationFunctionType
+ALU = mybir.AluOpType
+
+P = 128
+PASSES = K // 512
+HALF = 512
+WINDOW = V + HALF
+TINY = 2.0 ** -60
+
+
+def tile_picked_yjoinsz_rel_p_kernel(
+    tc, x_words, x_scales, w1_words, w1_scales, w2_words, w2_scales, sel, unit,
+    w3_words, w3_scales, offs, jn, qry, out,
+):
+    nc = tc.nc
+    with ExitStack() as ctx:
+        keep = ctx.enter_context(tc.tile_pool(name="keep", bufs=1))
+        early = ctx.enter_context(tc.tile_pool(name="early", bufs=1))
+        psum = ctx.enter_context(tc.psum_pool(name="psum", bufs=1))
+
+        offs_sb = keep.tile([P, S // 16], U16, name="offs_sb")
+        jn_sb = keep.tile([P, S // 16], U16, name="jn_sb")
+        qry_sb = keep.tile([P, U // 16], U16, name="qry_sb")
+        nc.sync.dma_start(offs_sb[:], offs)
+        nc.sync.dma_start(jn_sb[:], jn)
+        nc.sync.dma_start(qry_sb[:], qry)
+
+        x_table = []
+        for o in range(PASSES):
+            table = early.tile([P, T], I32, name="x_table%d" % o, align_bytes=64, offset=4 * T * o)
+            nc.sync.dma_start(table[:], x_words[o].rearrange("p n t -> p (n t)").bitcast(I32))
+            x_table.append(table)
+
+        xs_table = early.tile([P, PASSES, T], U8, name="xs_table", align_bytes=64, offset=8 * T)
+        nc.vector.memset(xs_table[:].bitcast(I32), 0)
+        w_raw = keep.tile([P, 2, PASSES, 2 * H], U8, name="w_raw", align_bytes=64)
+        for i, words in enumerate((w1_words, w2_words)):
+            nc.scalar.dma_start(w_raw[:, i].bitcast(I32), words.rearrange("o p c -> p o c").bitcast(I32))
+        for q in range(4):
+            nc.scalar.dma_start(
+                xs_table[32 * q:32 * q + 4].bitcast(I32),
+                x_scales[:, 4 * q:4 * q + 4, :].rearrange("o r c -> r o c").bitcast(I32))
+
+        ws_raw = keep.tile([P, 2, PASSES, H], U8, name="ws_raw", align_bytes=64)
+        unit2 = keep.tile([P, D], F32, name="unit2")
+        tiny = keep.tile([P, 1], F32, name="tiny")
+        nc.gpsimd.memset(ws_raw[:].bitcast(I32), 0)
+        for i, scales in enumerate((w1_scales, w2_scales)):
+            for q in range(4):
+                nc.gpsimd.dma_start(
+                    ws_raw[32 * q:32 * q + 4, i].bitcast(I32),
+                    scales[:, 4 * q:4 * q + 4, :].rearrange("o r c -> r o c").bitcast(I32))
+        nc.vector.memset(tiny[:], TINY)
+
+        w_dealt = [keep.tile([P, 2 * PASSES, P, 2], U8, name="w_dealt0", align_bytes=64)]
+        ws_dealt = [early.tile([P, 2 * PASSES, P], U8, name="ws_dealt0", align_bytes=64, offset=8 * T + T)]
+        for t in range(1, D):
+            w_dealt.append(early.tile([P, 2 * PASSES, P, 2], U8, name="w_dealt%d" % t, align_bytes=64, offset=4 * T + 8192 + 1536 * t))
+            ws_dealt.append(early.tile([P, 2 * PASSES, P], U8, name="ws_dealt%d" % t, align_bytes=64, offset=4 * T + 8192 + 1536 * t + 1024))
+
+        def deal_words(t):
+            src = w_raw[:].rearrange("p i o (m t b) -> p (i o) t m b", t=D, b=2)
+            nc.vector.tensor_copy(w_dealt[t][:].bitcast(U16), src[:, :, t].bitcast(U16))
+
+        def deal_scales(t):
+            src = ws_raw[:].rearrange("p i o (m t) -> p (i o) t m", t=D)
+            nc.vector.tensor_copy(ws_dealt[t][:], src[:, :, t])
+
+        xg = [[keep.tile([P, HALF], U32, name="xg%d_%d" % (o, h), align_bytes=64) for h in range(2)] for o in range(PASSES)]
+        xsg = [keep.tile([P, S], U8, name="xsg%d" % o, align_bytes=64) for o in range(PASSES)]
+
+        def gather_scales(o):
+            nc.vector.tensor_copy(xsg[o][:], xs_table[:, o].indirect(offs_sb[:]))
+
+        def gather_words(o, h):
+            nc.vector.tensor_copy(xg[o][h][:], x_table[o][:].bitcast(U32).indirect(offs_sb[:, 32 * h:32 * h + 32]))
+
+        deal_words(0)
+        gather_scales(0)
+        gather_words(0, 0)
+        gather_words(0, 1)
+        gather_scales(1)
+        deal_scales(0)
+        gather_words(1, 0)
+        gather_words(1, 1)
+        for t in range(1, D):
+            deal_words(t)
+            deal_scales(t)
+        w3w = early.tile([P, 2 * N], U8, name="w3w", align_bytes=64, offset=4 * T + 8192)
+        nc.sync.dma_start(w3w[:].bitcast(I32), w3_words[0].bitcast(I32))
+        unit_sb = early.tile([P, D], F32, name="unit_sb", align_bytes=64, offset=4 * T + 8192 + 512)
+        nc.sync.dma_start(unit_sb[:], unit.rearrange("(p t) one -> p (t one)", t=D))
+        w3s = early.tile([P, N], U8, name="w3s", align_bytes=64, offset=4 * T + 8192 + 1024)
+        nc.gpsimd.memset(w3s[:].bitcast(I32), 0)
+        for q in range(4):
+            nc.sync.dma_start(
+                w3s[32 * q:32 * q + 4].bitcast(I32), w3_scales[0, 4 * q:4 * q + 4, :].bitcast(I32))
+        nc.gpsimd.tensor_scalar(unit2[:], unit_sb[:], 2.0, 0.0, ALU.mult, ALU.add)
+
+        sel_sb = early.tile([P, D, U], F32, name="sel_sb", align_bytes=64, offset=4 * T)
+        nc.sync.dma_start(sel_sb[:], sel.rearrange("(p t) r -> p t r", t=D))
+
+        ring = [keep.tile([P, 5, S], F32, name="ring%d" % r) for r in range(2)]
+        banks = {}
+
+        def product(kind, t, h, slot):
+            acc = psum.tile([P, HALF], F32, name="acc", tag="bank%d" % (2 * slot + h))
+            for o in range(PASSES):
+                g = PASSES * kind + o
+                nc.tensor.matmul_mx(
+                    out=acc[:],
+                    lhsT=w_dealt[t][:, g].rearrange("p m b -> p (m b)").bitcast(FP4X4),
+                    lhsT_scale=ws_dealt[t][:, g],
+                    rhs=xg[o][h][:].bitcast(FP8X4),
+                    rhs_scale=xsg[o][:, HALF * h:HALF * (h + 1)],
+                    start=(o == 0), stop=(o == PASSES - 1))
+            banks[kind, t, h] = acc
+
+        place = {}
+
+        def sigmoid(kind, t, h):
+            r, i = place[kind, t]
+            nc.scalar.activation(ring[r][:, i + 1, HALF * h:HALF * (h + 1)], banks[kind, t, h][:], ACT.Sigmoid, scale=-1.0)
+
+        def log(kind, t):
+            r, i = place[kind, t]
+            nc.scalar.activation(ring[r][:, i], ring[r][:, i + 1], ACT.Ln, bias=tiny[:])
+
+        soft = {}
+
+        def softplus(kind, t):
+            r, i = place[kind, t]
+            tile = keep.tile([P, S], F32, name="soft%d_%d" % (kind, t))
+            for h in range(2):
+                cols = slice(HALF * h, HALF * (h + 1))
+                nc.vector.scalar_tensor_tensor(tile[:, cols], ring[r][:, i, cols], -1.0, banks[kind, t, h][:], ALU.mult, ALU.max)
+            soft[kind, t] = tile
+
+        recip_w = [keep.tile([P, WINDOW], F32, name="recip_w%d" % t) for t in range(D)]
+        ratio_w = [keep.tile([P, WINDOW], F32, name="ratio_w%d" % t) for t in range(D)]
+        heavy_late = keep.tile([P, 8, 64], F32, name="heavy_late")
+        heavy = [ring[1][:, 1:5].rearrange("p a (h c) -> p (a h) c", h=2)[:, :, 0:64], heavy_late[:]]
+        log_heavy = [keep.tile([P, 2 * V], F32, name="log_heavy%d" % r) for r in range(2)]
+
+        def largest(t):
+            f = soft[0, t]
+            pairs = recip_w[t][:, V:]
+            nc.vector.tensor_tensor(pairs, f[:, 0::2], f[:, 1::2], ALU.max)
+            pv = pairs.rearrange("p (a c e) -> p e a c", a=4, e=2)
+            dst = heavy[t // 2][:, 4 * (t % 2):4 * (t % 2) + 4]
+            nc.vector.scalar_tensor_tensor(dst, pv[:, 0], 0.0, pv[:, 1], ALU.max, ALU.max)
+
+        def log_of_heavy(r):
+            nc.scalar.activation(log_heavy[r][:].rearrange("p (a c) -> p a c", a=8), heavy[r], ACT.Ln, bias=tiny[:], scale=2.0)
+
+        def reciprocal(t):
+            cols = slice(V * (t % 2), V * (t % 2 + 1))
+            nc.scalar.activation(recip_w[t][:, 0:V], log_heavy[t // 2][:, cols], ACT.Sigmoid, scale=-1.0)
+
+        match = {}
+
+        def match_fused(t):
+            tile = keep.tile([P, S], F32, name="match%d" % t)
+            for h in range(2):
+                cols = slice(HALF * h, HALF * (h + 1))
+                nc.vector.tensor_tensor(tile[:, cols], soft[1, t][:].indirect(jn_sb[:, 32 * h:32 * h + 32]), soft[0, t][:, cols], ALU.mult)
+            match[t] = tile
+
+        partner = {}
+
+        def fetch_partner(t):
+            tile = keep.tile([P, S], F32, name="partner%d" % t)
+            for h in range(2):
+                cols = slice(HALF * h, HALF * (h + 1))
+                nc.scalar.activation(tile[:, cols], soft[1, t][:].indirect(jn_sb[:, 32 * h:32 * h + 32]), ACT.Copy)
+            partner[t] = tile
+
+        def match_plain(t):
+            tile = keep.tile([P, S], F32, name="match%d" % t)
+            nc.vector.tensor_tensor(tile[:], partner[t][:], soft[0, t][:], ALU.mult)
+            match[t] = tile
+
+        size = {}
+
+        def group_sum(t, dst):
+            pairs = ratio_w[t][:, V:]
+            nc.vector.tensor_tensor(pairs, match[t][:, 0::2], match[t][:, 1::2], ALU.add)
+            nc.vector.tensor_tensor(dst, pairs[:, 0::2], pairs[:, 1::2], ALU.add)
+            size[t] = dst
+
+        def ratio(t):
+            nc.vector.scalar_tensor_tensor(ratio_w[t][:, 0:V], size[t], unit2[:, t:t + 1], recip_w[t][:, 0:V], ALU.mult, ALU.mult)
+
+        term = keep.tile([P, D, U], F32, name="term")
+        recip_q = keep.tile([P, D, U], F32, name="recip_q")
+        hid = keep.tile([P, D, U], F32, name="hid")
+        sizes = keep.tile([P, D, V], F32, name="sizes")
+
+        def ratio_times_sel(t):
+            nc.vector.tensor_tensor(term[:, t], ratio_w[t][:].indirect(qry_sb[:]), sel_sb[:, t], ALU.mult)
+
+        def fetch_recip(t):
+            nc.scalar.activation(recip_q[:, t], recip_w[t][:].indirect(qry_sb[:]), ACT.Copy)
+
+        def hidden(t):
+            nc.vector.scalar_tensor_tensor(hid[:, t], recip_q[:, t], unit2[:, t:t + 1], term[:, t], ALU.mult, ALU.add)
+
+        logs = [(0, 1), (0, 0), (1, 1), (1, 0)]
+        for i, key in enumerate(logs):
+            place[key] = (0, i)
+        for kind, t, h in [(0, 0, 0), (1, 0, 0), (1, 0, 1), (0, 0, 1), (1, 1, 0), (1, 1, 1), (0, 1, 0), (0, 1, 1)]:
+            product(kind, t, h, place[kind, t][1])
+            sigmoid(kind, t, h)
+        for kind, t in logs:
+            log(kind, t)
+        for kind, t in logs:
+            softplus(kind, t)
+            if kind == 0:
+                largest(t)
+        log_of_heavy(0)
+        reciprocal(1)
+        reciprocal(0)
+
+        logs = [(1, 2), (1, 3), (0, 2), (0, 3)]
+        for i, key in enumerate(logs):
+            place[key] = (1, i)
+        for slot, (kind, t) in enumerate(logs[1:] + logs[:1]):
+            for h in range(2):
+                product(kind, t, h, slot)
+                sigmoid(kind, t, h)
+        match_fused(1)
+        group_sum(1, sizes[:, 1])
+        ratio(1)
+        ratio_times_sel(1)
+        match_fused(0)
+        for kind, t in logs:
+            log(kind, t)
+        for kind, t in logs:
+            softplus(kind, t)
+            if kind == 0:
+                largest(t)
+        fetch_partner(2)
+        fetch_partner(3)
+        log_of_heavy(1)
+        reciprocal(2)
+        reciprocal(3)
+        group_sum(0, ring[1][:, 3, 0:V])
+        ratio(0)
+        ratio_times_sel(0)
+        for t in (1, 0, 2, 3):
+            fetch_recip(t)
+        hidden(1)
+        hidden(0)
+        for t in (2, 3):
+            match_plain(t)
+            group_sum(t, sizes[:, t])
+        for t in (2, 3):
+            ratio(t)
+        for t in (2, 3):
+            ratio_times_sel(t)
+        for t in (2, 3):
+            hidden(t)
+
+        R = U // 2
+        grouped = []
+        for h in range(2):
+            tile = keep.tile([P, R, D], BF16, name="grouped%d" % h, align_bytes=64)
+            nc.vector.tensor_copy(
+                tile[:].rearrange("p (c i) t -> p c t i", i=4),
+                hid[:, :, R * h:R * (h + 1)].rearrange("p t (c i) -> p c t i", i=4))
+            grouped.append(tile)
+        for h in range(2):
+            codes = keep.tile([P, R], U32, name="codes%d" % h, align_bytes=64)
+            scales = keep.tile([P, R], U8, name="scales%d" % h, align_bytes=64)
+            nc.vector.quantize_mx(out=codes[:].bitcast(FP8X4), scales=scales[:], in_=grouped[h][:].rearrange("p r t -> p (r t)"))
+            for m in range(N // P):
+                acc = psum.tile([P, HALF], F32, name="acc", tag="bank%d" % (2 * h + m))
+                nc.tensor.matmul_mx(
+                    out=acc[:, 0:R],
+                    lhsT=w3w[:, 2 * P * m:2 * P * (m + 1)].bitcast(FP4X4),
+                    lhsT_scale=w3s[:, P * m:P * (m + 1)],
+                    rhs=codes[:].bitcast(FP8X4), rhs_scale=scales[:], start=True, stop=True)
+                res = keep.tile([P, R], F32, name="res%d_%d" % (h, m))
+                nc.scalar.copy(res[:], acc[:, 0:R])
+                nc.sync.dma_start(out[P * m:P * (m + 1), R * h:R * (h + 1)], res[:])

@@ -21,6 +21,10 @@ PASSES = K // 512
 HALF = 512
 WINDOW = V + HALF
 TINY = 2.0 ** -60
+X_TABLE = (0, 18432)
+WS_RAW = 16384
+XS_TABLE = 35840
+LATE = X_TABLE[1]
 
 
 def tile_picked_yjoinsz_rel_p_kernel(
@@ -42,24 +46,21 @@ def tile_picked_yjoinsz_rel_p_kernel(
 
         x_table = []
         for o in range(PASSES):
-            table = early.tile([P, T], I32, name="x_table%d" % o, align_bytes=64, offset=4 * T * o)
+            table = early.tile([P, T], I32, name="x_table%d" % o, align_bytes=64, offset=X_TABLE[o])
             nc.sync.dma_start(table[:], x_words[o].rearrange("p n t -> p (n t)").bitcast(I32))
             x_table.append(table)
 
-        xs_table = early.tile([P, PASSES, T], U8, name="xs_table", align_bytes=64, offset=8 * T)
+        xs_table = early.tile([P, T], U8, name="xs_table", align_bytes=64, offset=XS_TABLE)
         nc.vector.memset(xs_table[:].bitcast(I32), 0)
+        ws_raw = early.tile([P, 2, PASSES, H], U8, name="ws_raw", align_bytes=64, offset=WS_RAW)
+        nc.vector.memset(ws_raw[:].bitcast(I32), 0)
         w_raw = keep.tile([P, 2, PASSES, 2 * H], U8, name="w_raw", align_bytes=64)
         for i, words in enumerate((w1_words, w2_words)):
             nc.scalar.dma_start(w_raw[:, i].bitcast(I32), words.rearrange("o p c -> p o c").bitcast(I32))
-        for q in range(4):
-            nc.scalar.dma_start(
-                xs_table[32 * q:32 * q + 4].bitcast(I32),
-                x_scales[:, 4 * q:4 * q + 4, :].rearrange("o r c -> r o c").bitcast(I32))
+        nc.scalar.dma_start(xs_table[0:32].bitcast(I32), x_scales.rearrange("o q c -> (o q) c").bitcast(I32))
 
-        ws_raw = keep.tile([P, 2, PASSES, H], U8, name="ws_raw", align_bytes=64)
         unit2 = keep.tile([P, D], F32, name="unit2")
         tiny = keep.tile([P, 1], F32, name="tiny")
-        nc.gpsimd.memset(ws_raw[:].bitcast(I32), 0)
         for i, scales in enumerate((w1_scales, w2_scales)):
             for q in range(4):
                 nc.gpsimd.dma_start(
@@ -68,68 +69,77 @@ def tile_picked_yjoinsz_rel_p_kernel(
         nc.vector.memset(tiny[:], TINY)
 
         w_dealt = [keep.tile([P, 2 * PASSES, P, 2], U8, name="w_dealt0", align_bytes=64)]
-        ws_dealt = [early.tile([P, 2 * PASSES, P], U8, name="ws_dealt0", align_bytes=64, offset=8 * T + T)]
+        ws_dealt = early.tile([P, D, 2 * PASSES, P], U8, name="ws_dealt", align_bytes=64, offset=0)
         for t in range(1, D):
-            w_dealt.append(early.tile([P, 2 * PASSES, P, 2], U8, name="w_dealt%d" % t, align_bytes=64, offset=4 * T + 8192 + 1536 * t))
-            ws_dealt.append(early.tile([P, 2 * PASSES, P], U8, name="ws_dealt%d" % t, align_bytes=64, offset=4 * T + 8192 + 1536 * t + 1024))
+            w_dealt.append(early.tile([P, 2 * PASSES, P, 2], U8, name="w_dealt%d" % t, align_bytes=64, offset=XS_TABLE + 1024 if t == 1 else LATE + 10240 + 1024 * t))
 
         def deal_words(t):
             src = w_raw[:].rearrange("p i o (m t b) -> p (i o) t m b", t=D, b=2)
             nc.vector.tensor_copy(w_dealt[t][:].bitcast(U16), src[:, :, t].bitcast(U16))
 
-        def deal_scales(t):
-            src = ws_raw[:].rearrange("p i o (m t) -> p (i o) t m", t=D)
-            nc.vector.tensor_copy(ws_dealt[t][:], src[:, :, t])
+        def deal_scales(i):
+            nc.vector.tensor_copy(ws_dealt[:, :, PASSES * i:PASSES * (i + 1)].rearrange("p t g m -> p (g m) t"), ws_raw[:, i].rearrange("p o (m t) -> p (o m) t", t=D))
 
-        xg = [[keep.tile([P, HALF], U32, name="xg%d_%d" % (o, h), align_bytes=64) for h in range(2)] for o in range(PASSES)]
-        xsg = [keep.tile([P, S], U8, name="xsg%d" % o, align_bytes=64) for o in range(PASSES)]
+        xg1 = early.tile([P, S], U32, name="xg1", align_bytes=64, offset=WS_RAW - 2048)
+        xg = [[early.tile([P, HALF], U32, name="xg0_%d" % h, align_bytes=64, offset=XS_TABLE - 1024 + 4096 * h) for h in range(2)],
+              [xg1[:, 0:HALF], xg1[:, HALF:S]]]
+        xs_picked = keep.tile([P, S], U8, name="xs_picked", align_bytes=64)
+        xsg = keep.tile([P, PASSES, S], U8, name="xsg", align_bytes=64)
 
-        def gather_scales(o):
-            nc.vector.tensor_copy(xsg[o][:], xs_table[:, o].indirect(offs_sb[:]))
+        nc.vector.memset(xsg[:].bitcast(I32), 0)
+
+        def gather_scales():
+            nc.vector.tensor_copy(xs_picked[:], xs_table[:].indirect(offs_sb[:]))
+            for o in range(PASSES):
+                for q in range(4):
+                    queue = nc.gpsimd if q == 3 else nc.scalar
+                    row = 16 * o + 4 * q
+                    queue.dma_start(xsg[32 * q:32 * q + 4, o].bitcast(I32), xs_picked[row:row + 4].bitcast(I32))
 
         def gather_words(o, h):
             nc.vector.tensor_copy(xg[o][h][:], x_table[o][:].bitcast(U32).indirect(offs_sb[:, 32 * h:32 * h + 32]))
 
         deal_words(0)
-        gather_scales(0)
+        gather_scales()
+        deal_words(1)
         gather_words(0, 0)
         gather_words(0, 1)
-        gather_scales(1)
         deal_scales(0)
+        deal_scales(1)
         gather_words(1, 0)
         gather_words(1, 1)
-        for t in range(1, D):
+        for t in range(2, D):
             deal_words(t)
-            deal_scales(t)
-        w3w = early.tile([P, 2 * N], U8, name="w3w", align_bytes=64, offset=4 * T + 8192)
+        w3w = early.tile([P, 2 * N], U8, name="w3w", align_bytes=64, offset=LATE + 8192)
         nc.sync.dma_start(w3w[:].bitcast(I32), w3_words[0].bitcast(I32))
-        unit_sb = early.tile([P, D], F32, name="unit_sb", align_bytes=64, offset=4 * T + 8192 + 512)
+        unit_sb = early.tile([P, D], F32, name="unit_sb", align_bytes=64, offset=LATE + 8192 + 512)
         nc.sync.dma_start(unit_sb[:], unit.rearrange("(p t) one -> p (t one)", t=D))
-        w3s = early.tile([P, N], U8, name="w3s", align_bytes=64, offset=4 * T + 8192 + 1024)
+        w3s = early.tile([P, N], U8, name="w3s", align_bytes=64, offset=LATE + 8192 + 1024)
         nc.gpsimd.memset(w3s[:].bitcast(I32), 0)
         for q in range(4):
             nc.sync.dma_start(
                 w3s[32 * q:32 * q + 4].bitcast(I32), w3_scales[0, 4 * q:4 * q + 4, :].bitcast(I32))
         nc.gpsimd.tensor_scalar(unit2[:], unit_sb[:], 2.0, 0.0, ALU.mult, ALU.add)
 
-        sel_sb = early.tile([P, D, U], F32, name="sel_sb", align_bytes=64, offset=4 * T)
+        sel_sb = early.tile([P, D, U], F32, name="sel_sb", align_bytes=64, offset=LATE)
         nc.sync.dma_start(sel_sb[:], sel.rearrange("(p t) r -> p t r", t=D))
 
         ring = [keep.tile([P, 5, S], F32, name="ring%d" % r) for r in range(2)]
         banks = {}
 
-        def product(kind, t, h, slot):
-            acc = psum.tile([P, HALF], F32, name="acc", tag="bank%d" % (2 * slot + h))
-            for o in range(PASSES):
+        def product(kind, t, h, slot, passes=range(PASSES)):
+            if 0 in passes:
+                banks[kind, t, h] = psum.tile([P, HALF], F32, name="acc", tag="bank%d" % (2 * slot + h))
+            acc = banks[kind, t, h]
+            for o in passes:
                 g = PASSES * kind + o
                 nc.tensor.matmul_mx(
                     out=acc[:],
                     lhsT=w_dealt[t][:, g].rearrange("p m b -> p (m b)").bitcast(FP4X4),
-                    lhsT_scale=ws_dealt[t][:, g],
+                    lhsT_scale=ws_dealt[:, t, g],
                     rhs=xg[o][h][:].bitcast(FP8X4),
-                    rhs_scale=xsg[o][:, HALF * h:HALF * (h + 1)],
+                    rhs_scale=xsg[:, o, HALF * h:HALF * (h + 1)],
                     start=(o == 0), stop=(o == PASSES - 1))
-            banks[kind, t, h] = acc
 
         place = {}
 
@@ -143,13 +153,14 @@ def tile_picked_yjoinsz_rel_p_kernel(
 
         soft = {}
 
-        def softplus(kind, t):
+        for kind in range(2):
+            for t in range(D):
+                soft[kind, t] = keep.tile([P, S], F32, name="soft%d_%d" % (kind, t))
+
+        def softplus(kind, t, h):
             r, i = place[kind, t]
-            tile = keep.tile([P, S], F32, name="soft%d_%d" % (kind, t))
-            for h in range(2):
-                cols = slice(HALF * h, HALF * (h + 1))
-                nc.vector.scalar_tensor_tensor(tile[:, cols], ring[r][:, i, cols], -1.0, banks[kind, t, h][:], ALU.mult, ALU.max)
-            soft[kind, t] = tile
+            cols = slice(HALF * h, HALF * (h + 1))
+            nc.vector.scalar_tensor_tensor(soft[kind, t][:, cols], ring[r][:, i, cols], -1.0, banks[kind, t, h][:], ALU.mult, ALU.max)
 
         recip_w = [keep.tile([P, WINDOW], F32, name="recip_w%d" % t) for t in range(D)]
         ratio_w = [keep.tile([P, WINDOW], F32, name="ratio_w%d" % t) for t in range(D)]
@@ -157,10 +168,12 @@ def tile_picked_yjoinsz_rel_p_kernel(
         heavy = [ring[1][:, 1:5].rearrange("p a (h c) -> p (a h) c", h=2)[:, :, 0:64], heavy_late[:]]
         log_heavy = [keep.tile([P, 2 * V], F32, name="log_heavy%d" % r) for r in range(2)]
 
-        def largest(t):
+        def pair_largest(t):
             f = soft[0, t]
+            nc.vector.tensor_tensor(recip_w[t][:, V:], f[:, 0::2], f[:, 1::2], ALU.max)
+
+        def largest(t):
             pairs = recip_w[t][:, V:]
-            nc.vector.tensor_tensor(pairs, f[:, 0::2], f[:, 1::2], ALU.max)
             pv = pairs.rearrange("p (a c e) -> p e a c", a=4, e=2)
             dst = heavy[t // 2][:, 4 * (t % 2):4 * (t % 2) + 4]
             nc.vector.scalar_tensor_tensor(dst, pv[:, 0], 0.0, pv[:, 1], ALU.max, ALU.max)
@@ -172,14 +185,11 @@ def tile_picked_yjoinsz_rel_p_kernel(
             cols = slice(V * (t % 2), V * (t % 2 + 1))
             nc.scalar.activation(recip_w[t][:, 0:V], log_heavy[t // 2][:, cols], ACT.Sigmoid, scale=-1.0)
 
-        match = {}
+        match = [keep.tile([P, S], F32, name="match%d" % t) for t in range(D)]
 
-        def match_fused(t):
-            tile = keep.tile([P, S], F32, name="match%d" % t)
-            for h in range(2):
-                cols = slice(HALF * h, HALF * (h + 1))
-                nc.vector.tensor_tensor(tile[:, cols], soft[1, t][:].indirect(jn_sb[:, 32 * h:32 * h + 32]), soft[0, t][:, cols], ALU.mult)
-            match[t] = tile
+        def match_fused(t, h):
+            cols = slice(HALF * h, HALF * (h + 1))
+            nc.vector.tensor_tensor(match[t][:, cols], soft[1, t][:].indirect(jn_sb[:, 32 * h:32 * h + 32]), soft[0, t][:, cols], ALU.mult)
 
         partner = {}
 
@@ -191,47 +201,67 @@ def tile_picked_yjoinsz_rel_p_kernel(
             partner[t] = tile
 
         def match_plain(t):
-            tile = keep.tile([P, S], F32, name="match%d" % t)
-            nc.vector.tensor_tensor(tile[:], partner[t][:], soft[0, t][:], ALU.mult)
-            match[t] = tile
+            nc.vector.tensor_tensor(match[t][:], partner[t][:], soft[0, t][:], ALU.mult)
 
-        size = {}
+        def pair_sum(t):
+            nc.vector.tensor_tensor(ratio_w[t][:, V:], match[t][:, 0::2], match[t][:, 1::2], ALU.add)
 
-        def group_sum(t, dst):
+        def group_sum(t):
             pairs = ratio_w[t][:, V:]
-            nc.vector.tensor_tensor(pairs, match[t][:, 0::2], match[t][:, 1::2], ALU.add)
-            nc.vector.tensor_tensor(dst, pairs[:, 0::2], pairs[:, 1::2], ALU.add)
-            size[t] = dst
+            nc.vector.tensor_tensor(sizes[:, t], pairs[:, 0::2], pairs[:, 1::2], ALU.add)
 
         def ratio(t):
-            nc.vector.scalar_tensor_tensor(ratio_w[t][:, 0:V], size[t], unit2[:, t:t + 1], recip_w[t][:, 0:V], ALU.mult, ALU.mult)
+            nc.vector.scalar_tensor_tensor(ratio_w[t][:, 0:V], sizes[:, t], unit2[:, t:t + 1], recip_w[t][:, 0:V], ALU.mult, ALU.mult)
 
-        term = keep.tile([P, D, U], F32, name="term")
+        term_rest = keep.tile([P, D, U], F32, name="term_rest")
+        term = [ring[1][:, 1, 0:U], term_rest[:, 1], term_rest[:, 2], term_rest[:, 3]]
         recip_q = keep.tile([P, D, U], F32, name="recip_q")
         hid = keep.tile([P, D, U], F32, name="hid")
         sizes = keep.tile([P, D, V], F32, name="sizes")
 
         def ratio_times_sel(t):
-            nc.vector.tensor_tensor(term[:, t], ratio_w[t][:].indirect(qry_sb[:]), sel_sb[:, t], ALU.mult)
+            nc.vector.tensor_tensor(term[t], ratio_w[t][:].indirect(qry_sb[:]), sel_sb[:, t], ALU.mult)
 
         def fetch_recip(t):
             nc.scalar.activation(recip_q[:, t], recip_w[t][:].indirect(qry_sb[:]), ACT.Copy)
 
         def hidden(t):
-            nc.vector.scalar_tensor_tensor(hid[:, t], recip_q[:, t], unit2[:, t:t + 1], term[:, t], ALU.mult, ALU.add)
+            nc.vector.scalar_tensor_tensor(hid[:, t], recip_q[:, t], unit2[:, t:t + 1], term[t], ALU.mult, ALU.add)
+
+        def fetch_ratio(t):
+            nc.scalar.activation(term_rest[:, 0], ratio_w[t][:].indirect(qry_sb[:]), ACT.Copy)
+
+        def fetched_times_sel(t):
+            nc.vector.tensor_tensor(term[t], term_rest[:, 0], sel_sb[:, t], ALU.mult)
 
         logs = [(0, 1), (0, 0), (1, 1), (1, 0)]
         for i, key in enumerate(logs):
             place[key] = (0, i)
-        for kind, t, h in [(0, 0, 0), (1, 0, 0), (1, 0, 1), (0, 0, 1), (1, 1, 0), (1, 1, 1), (0, 1, 0), (0, 1, 1)]:
-            product(kind, t, h, place[kind, t][1])
-            sigmoid(kind, t, h)
+        for kind, t in logs:
+            product(kind, t, 0, place[kind, t][1], [0])
+        for kind, t in logs:
+            product(kind, t, 0, place[kind, t][1], [1])
+            sigmoid(kind, t, 0)
+        for kind, t in reversed(logs):
+            product(kind, t, 1, place[kind, t][1])
+            sigmoid(kind, t, 1)
         for kind, t in logs:
             log(kind, t)
-        for kind, t in logs:
-            softplus(kind, t)
-            if kind == 0:
-                largest(t)
+        def softplus_and_largest(a, b):
+            softplus(0, a, 0)
+            softplus(0, a, 1)
+            softplus(0, b, 0)
+            pair_largest(a)
+            softplus(0, b, 1)
+            largest(a)
+            pair_largest(b)
+
+        softplus_and_largest(1, 0)
+        softplus(1, 1, 0)
+        largest(0)
+        softplus(1, 1, 1)
+        softplus(1, 0, 0)
+        softplus(1, 0, 1)
         log_of_heavy(0)
         reciprocal(1)
         reciprocal(0)
@@ -243,44 +273,54 @@ def tile_picked_yjoinsz_rel_p_kernel(
             for h in range(2):
                 product(kind, t, h, slot)
                 sigmoid(kind, t, h)
-        match_fused(1)
-        group_sum(1, sizes[:, 1])
+        match_fused(1, 0)
+        match_fused(1, 1)
+        match_fused(0, 0)
+        pair_sum(1)
+        match_fused(0, 1)
+        group_sum(1)
+        pair_sum(0)
         ratio(1)
+        group_sum(0)
         ratio_times_sel(1)
-        match_fused(0)
+        ratio(0)
         for kind, t in logs:
             log(kind, t)
-        for kind, t in logs:
-            softplus(kind, t)
-            if kind == 0:
-                largest(t)
+        for t in (2, 3):
+            for h in range(2):
+                softplus(1, t, h)
         fetch_partner(2)
         fetch_partner(3)
+        softplus_and_largest(2, 3)
+        ratio_times_sel(0)
+        largest(3)
         log_of_heavy(1)
         reciprocal(2)
         reciprocal(3)
-        group_sum(0, ring[1][:, 3, 0:V])
-        ratio(0)
-        ratio_times_sel(0)
         for t in (1, 0, 2, 3):
             fetch_recip(t)
+        match_plain(2)
+        match_plain(3)
+        pair_sum(2)
+        pair_sum(3)
+        group_sum(2)
+        group_sum(3)
         hidden(1)
+        ratio(3)
+        ratio(2)
+        fetch_ratio(3)
         hidden(0)
-        for t in (2, 3):
-            match_plain(t)
-            group_sum(t, sizes[:, t])
-        for t in (2, 3):
-            ratio(t)
-        for t in (2, 3):
-            ratio_times_sel(t)
-        for t in (2, 3):
-            hidden(t)
+        ratio_times_sel(2)
+        fetched_times_sel(3)
+        hidden(2)
+        hidden(3)
 
         R = U // 2
         grouped = []
         for h in range(2):
             tile = keep.tile([P, R, D], BF16, name="grouped%d" % h, align_bytes=64)
-            nc.vector.tensor_copy(
+            copy = nc.vector.tensor_copy if h == 0 else nc.scalar.copy
+            copy(
                 tile[:].rearrange("p (c i) t -> p c t i", i=4),
                 hid[:, :, R * h:R * (h + 1)].rearrange("p t (c i) -> p c t i", i=4))
             grouped.append(tile)
@@ -296,5 +336,6 @@ def tile_picked_yjoinsz_rel_p_kernel(
                     lhsT_scale=w3s[:, P * m:P * (m + 1)],
                     rhs=codes[:].bitcast(FP8X4), rhs_scale=scales[:], start=True, stop=True)
                 res = keep.tile([P, R], F32, name="res%d_%d" % (h, m))
-                nc.scalar.copy(res[:], acc[:, 0:R])
+                copy = nc.vector.tensor_copy if (h, m) == (1, 1) else nc.scalar.copy
+                copy(res[:], acc[:, 0:R])
                 nc.sync.dma_start(out[P * m:P * (m + 1), R * h:R * (h + 1)], res[:])

@@ -21,9 +21,9 @@ PASSES = K // 512
 HALF = 512
 WINDOW = V + HALF
 TINY = 2.0 ** -60
-X_TABLE = (0, 18432)
-WS_RAW = 16384
-XS_TABLE = 35840
+X_TABLE = (0, 16384)
+WS_RAW = 32768
+XS_TABLE = 34816
 LATE = X_TABLE[1]
 
 
@@ -47,7 +47,7 @@ def tile_picked_yjoinsz_rel_p_kernel(
         x_table = []
         for o in range(PASSES):
             table = early.tile([P, T], I32, name="x_table%d" % o, align_bytes=64, offset=X_TABLE[o])
-            nc.sync.dma_start(table[:], x_words[o].rearrange("p n t -> p (n t)").bitcast(I32))
+            nc.gpsimd.dma_start(table[:], x_words[o].rearrange("p n t -> p (n t)").bitcast(I32))
             x_table.append(table)
 
         xs_table = early.tile([P, T], U8, name="xs_table", align_bytes=64, offset=XS_TABLE)
@@ -63,15 +63,15 @@ def tile_picked_yjoinsz_rel_p_kernel(
         tiny = keep.tile([P, 1], F32, name="tiny")
         for i, scales in enumerate((w1_scales, w2_scales)):
             for q in range(4):
-                nc.gpsimd.dma_start(
+                nc.sync.dma_start(
                     ws_raw[32 * q:32 * q + 4, i].bitcast(I32),
                     scales[:, 4 * q:4 * q + 4, :].rearrange("o r c -> r o c").bitcast(I32))
         nc.vector.memset(tiny[:], TINY)
 
         w_dealt = [keep.tile([P, 2 * PASSES, P, 2], U8, name="w_dealt0", align_bytes=64)]
-        ws_dealt = early.tile([P, D, 2 * PASSES, P], U8, name="ws_dealt", align_bytes=64, offset=0)
+        ws_dealt = early.tile([P, D, 2 * PASSES, P], U8, name="ws_dealt", align_bytes=64, offset=XS_TABLE + 5120)
         for t in range(1, D):
-            w_dealt.append(early.tile([P, 2 * PASSES, P, 2], U8, name="w_dealt%d" % t, align_bytes=64, offset=XS_TABLE + 1024 if t == 1 else LATE + 10240 + 1024 * t))
+            w_dealt.append(early.tile([P, 2 * PASSES, P, 2], U8, name="w_dealt%d" % t, align_bytes=64, offset=XS_TABLE + 3072 if t == 1 else LATE + 10240 + 1024 * t))
 
         def deal_words(t):
             src = w_raw[:].rearrange("p i o (m t b) -> p (i o) t m b", t=D, b=2)
@@ -80,8 +80,9 @@ def tile_picked_yjoinsz_rel_p_kernel(
         def deal_scales(i):
             nc.vector.tensor_copy(ws_dealt[:, :, PASSES * i:PASSES * (i + 1)].rearrange("p t g m -> p (g m) t"), ws_raw[:, i].rearrange("p o (m t) -> p (o m) t", t=D))
 
-        xg1 = early.tile([P, S], U32, name="xg1", align_bytes=64, offset=WS_RAW - 2048)
-        xg = [[early.tile([P, HALF], U32, name="xg0_%d" % h, align_bytes=64, offset=XS_TABLE - 1024 + 4096 * h) for h in range(2)],
+        xg1 = early.tile([P, S], U32, name="xg1", align_bytes=64, offset=0)
+        xg0 = early.tile([P, S], U32, name="xg0", align_bytes=64, offset=XS_TABLE - 1024)
+        xg = [[xg0[:, 0:HALF], xg0[:, HALF:S]],
               [xg1[:, 0:HALF], xg1[:, HALF:S]]]
         xs_picked = keep.tile([P, S], U8, name="xs_picked", align_bytes=64)
         xsg = keep.tile([P, PASSES, S], U8, name="xsg", align_bytes=64)
@@ -92,9 +93,8 @@ def tile_picked_yjoinsz_rel_p_kernel(
             nc.vector.tensor_copy(xs_picked[:], xs_table[:].indirect(offs_sb[:]))
             for o in range(PASSES):
                 for q in range(4):
-                    queue = nc.gpsimd if q == 3 else nc.scalar
                     row = 16 * o + 4 * q
-                    queue.dma_start(xsg[32 * q:32 * q + 4, o].bitcast(I32), xs_picked[row:row + 4].bitcast(I32))
+                    nc.sync.dma_start(xsg[32 * q:32 * q + 4, o].bitcast(I32), xs_picked[row:row + 4].bitcast(I32))
 
         def gather_words(o, h):
             nc.vector.tensor_copy(xg[o][h][:], x_table[o][:].bitcast(U32).indirect(offs_sb[:, 32 * h:32 * h + 32]))
@@ -102,10 +102,10 @@ def tile_picked_yjoinsz_rel_p_kernel(
         deal_words(0)
         gather_scales()
         deal_words(1)
-        gather_words(0, 0)
-        gather_words(0, 1)
         deal_scales(0)
         deal_scales(1)
+        gather_words(0, 0)
+        gather_words(0, 1)
         gather_words(1, 0)
         gather_words(1, 1)
         for t in range(2, D):
@@ -124,7 +124,7 @@ def tile_picked_yjoinsz_rel_p_kernel(
         sel_sb = early.tile([P, D, U], F32, name="sel_sb", align_bytes=64, offset=LATE)
         nc.sync.dma_start(sel_sb[:], sel.rearrange("(p t) r -> p t r", t=D))
 
-        ring = [keep.tile([P, 5, S], F32, name="ring%d" % r) for r in range(2)]
+        ring = [keep.tile([P, 5 + r, S], F32, name="ring%d" % r) for r in range(2)]
         banks = {}
 
         def product(kind, t, h, slot, passes=range(PASSES)):
@@ -145,11 +145,14 @@ def tile_picked_yjoinsz_rel_p_kernel(
 
         def sigmoid(kind, t, h):
             r, i = place[kind, t]
-            nc.scalar.activation(ring[r][:, i + 1, HALF * h:HALF * (h + 1)], banks[kind, t, h][:], ACT.Sigmoid, scale=-1.0)
+            nc.scalar.activation(ring[r][:, i + 1 + r, HALF * h:HALF * (h + 1)], banks[kind, t, h][:], ACT.Sigmoid, scale=-1.0)
 
         def log(kind, t):
             r, i = place[kind, t]
             nc.scalar.activation(ring[r][:, i], ring[r][:, i + 1], ACT.Ln, bias=tiny[:])
+
+        def log_pair(r, i):
+            nc.scalar.activation(ring[r][:, i:i + 2], ring[r][:, i + 2:i + 4], ACT.Ln, bias=tiny[:])
 
         soft = {}
 
@@ -165,7 +168,7 @@ def tile_picked_yjoinsz_rel_p_kernel(
         recip_w = [keep.tile([P, WINDOW], F32, name="recip_w%d" % t) for t in range(D)]
         ratio_w = [keep.tile([P, WINDOW], F32, name="ratio_w%d" % t) for t in range(D)]
         heavy_late = keep.tile([P, 8, 64], F32, name="heavy_late")
-        heavy = [ring[1][:, 1:5].rearrange("p a (h c) -> p (a h) c", h=2)[:, :, 0:64], heavy_late[:]]
+        heavy = [ring[1][:, 2:6].rearrange("p a (h c) -> p (a h) c", h=2)[:, :, 0:64], heavy_late[:]]
         log_heavy = [keep.tile([P, 2 * V], F32, name="log_heavy%d" % r) for r in range(2)]
 
         def pair_largest(t):
@@ -214,25 +217,37 @@ def tile_picked_yjoinsz_rel_p_kernel(
             nc.vector.scalar_tensor_tensor(ratio_w[t][:, 0:V], sizes[:, t], unit2[:, t:t + 1], recip_w[t][:, 0:V], ALU.mult, ALU.mult)
 
         term_rest = keep.tile([P, D, U], F32, name="term_rest")
-        term = [ring[1][:, 1, 0:U], term_rest[:, 1], term_rest[:, 2], term_rest[:, 3]]
-        recip_q = keep.tile([P, D, U], F32, name="recip_q")
+        term = [ring[1][:, 3, HALF:S], term_rest[:, 1], term_rest[:, 2], term_rest[:, 3]]
+        recip_late = keep.tile([P, 2, U], F32, name="recip_late")
+        recip_q = [ring[1][:, 5, 0:U], ring[1][:, 5, U:2 * U], recip_late[:, 0], recip_late[:, 1]]
         hid = keep.tile([P, D, U], F32, name="hid")
         sizes = keep.tile([P, D, V], F32, name="sizes")
 
-        def ratio_times_sel(t):
-            nc.vector.tensor_tensor(term[t], ratio_w[t][:].indirect(qry_sb[:]), sel_sb[:, t], ALU.mult)
+        ratio_late = keep.tile([P, 2, U], F32, name="ratio_late")
+        ratio_q = [ring[1][:, 4, 0:U], ring[1][:, 4, U:2 * U], ratio_late[:, 0], ratio_late[:, 1]]
 
-        def fetch_recip(t):
-            nc.scalar.activation(recip_q[:, t], recip_w[t][:].indirect(qry_sb[:]), ACT.Copy)
+        def ratio_times_sel(t, a=0, b=U):
+            nc.vector.tensor_tensor(term[t][:, a:b], ratio_w[t][:].indirect(qry_sb[:, a // 16:b // 16]), sel_sb[:, t, a:b], ALU.mult)
 
-        def hidden(t):
-            nc.vector.scalar_tensor_tensor(hid[:, t], recip_q[:, t], unit2[:, t:t + 1], term[t], ALU.mult, ALU.add)
+        def fetch_recip(t, a=0, b=U):
+            nc.scalar.activation(recip_q[t][:, a:b], recip_w[t][:].indirect(qry_sb[:, a // 16:b // 16]), ACT.Copy)
 
-        def fetch_ratio(t):
-            nc.scalar.activation(term_rest[:, 0], ratio_w[t][:].indirect(qry_sb[:]), ACT.Copy)
+        def hidden(t, a=0, b=U):
+            nc.vector.scalar_tensor_tensor(hid[:, t, a:b], recip_q[t][:, a:b], unit2[:, t:t + 1], term[t][:, a:b], ALU.mult, ALU.add)
 
-        def fetched_times_sel(t):
-            nc.vector.tensor_tensor(term[t], term_rest[:, 0], sel_sb[:, t], ALU.mult)
+        def fetch_ratio(t, a=0, b=U):
+            nc.scalar.activation(ratio_q[t][:, a:b], ratio_w[t][:].indirect(qry_sb[:, a // 16:b // 16]), ACT.Copy)
+
+        def fetched_times_sel(t, a=0, b=U):
+            nc.vector.tensor_tensor(term[t][:, a:b], ratio_q[t][:, a:b], sel_sb[:, t, a:b], ALU.mult)
+
+        R = U // 2
+        grouped = [keep.tile([P, R, D], BF16, name="grouped%d" % h, align_bytes=64) for h in range(2)]
+
+        def interleave(h):
+            copy = nc.scalar.copy if h == 0 else nc.vector.tensor_copy
+            copy(grouped[h][:].rearrange("p (c i) t -> p c t i", i=4),
+                 hid[:, :, R * h:R * (h + 1)].rearrange("p t (c i) -> p c t i", i=4))
 
         logs = [(0, 1), (0, 0), (1, 1), (1, 0)]
         for i, key in enumerate(logs):
@@ -269,7 +284,7 @@ def tile_picked_yjoinsz_rel_p_kernel(
         logs = [(1, 2), (1, 3), (0, 2), (0, 3)]
         for i, key in enumerate(logs):
             place[key] = (1, i)
-        for slot, (kind, t) in enumerate(logs[1:] + logs[:1]):
+        for slot, (kind, t) in enumerate(logs[2:] + logs[:2]):
             for h in range(2):
                 product(kind, t, h, slot)
                 sigmoid(kind, t, h)
@@ -284,8 +299,8 @@ def tile_picked_yjoinsz_rel_p_kernel(
         group_sum(0)
         ratio_times_sel(1)
         ratio(0)
-        for kind, t in logs:
-            log(kind, t)
+        log_pair(1, 0)
+        log_pair(1, 2)
         for t in (2, 3):
             for h in range(2):
                 softplus(1, t, h)
@@ -297,8 +312,11 @@ def tile_picked_yjoinsz_rel_p_kernel(
         log_of_heavy(1)
         reciprocal(2)
         reciprocal(3)
-        for t in (1, 0, 2, 3):
+        for t in (1, 0):
             fetch_recip(t)
+        for a in (0, 256):
+            for t in (2, 3):
+                fetch_recip(t, a, a + 256)
         match_plain(2)
         match_plain(3)
         pair_sum(2)
@@ -308,22 +326,18 @@ def tile_picked_yjoinsz_rel_p_kernel(
         hidden(1)
         ratio(3)
         ratio(2)
-        fetch_ratio(3)
         hidden(0)
-        ratio_times_sel(2)
-        fetched_times_sel(3)
-        hidden(2)
-        hidden(3)
+        for a in (0, 256):
+            if a:
+                fetch_ratio(3, a, a + 256)
+                fetched_times_sel(3, a, a + 256)
+            else:
+                ratio_times_sel(3, a, a + 256)
+            ratio_times_sel(2, a, a + 256)
+            hidden(3, a, a + 256)
+            hidden(2, a, a + 256)
+            interleave(a // 256)
 
-        R = U // 2
-        grouped = []
-        for h in range(2):
-            tile = keep.tile([P, R, D], BF16, name="grouped%d" % h, align_bytes=64)
-            copy = nc.vector.tensor_copy if h == 0 else nc.scalar.copy
-            copy(
-                tile[:].rearrange("p (c i) t -> p c t i", i=4),
-                hid[:, :, R * h:R * (h + 1)].rearrange("p t (c i) -> p c t i", i=4))
-            grouped.append(tile)
         for h in range(2):
             codes = keep.tile([P, R], U32, name="codes%d" % h, align_bytes=64)
             scales = keep.tile([P, R], U8, name="scales%d" % h, align_bytes=64)

@@ -2,7 +2,7 @@ from contextlib import ExitStack
 
 import concourse.mybir as mybir
 
-K, T, S, D, N, H, V, U = 1024, 4096, 1024, 4, 256, 512, 256, 512
+K, T, S, N, H, V, U = 1024, 4096, 1024, 256, 512, 256, 512
 FLOPS = 2 * (2 * K * H * S + H * N * U)
 
 F32 = mybir.dt.float32
@@ -17,14 +17,36 @@ ACT = mybir.ActivationFunctionType
 ALU = mybir.AluOpType
 
 P = 128
-PASSES = K // 512
-HALF = 512
-WINDOW = V + HALF
+PACK = 4
+PASSES = K // (P * PACK)
+QUADRANTS = 4
+BANK = 512
+PER_COLUMN = 16
+HALF_U = U // 2
+WINDOW = V + S // 2
 TINY = 2.0 ** -60
-X_TABLE = (0, 16384)
-WS_RAW = 32768
-XS_TABLE = 34816
-LATE = X_TABLE[1]
+FREQ, FRQ2 = 0, 1
+
+SCALE_LOADS_ON_SCALAR = 5
+
+KIB = 1024
+AT_X_TABLE = (0, 16 * KIB)
+AT_WS_RAW = 35 * KIB
+AT_XS_TABLE = 45 * KIB
+AT_UNIT = AT_X_TABLE[1]
+AT_X_PICKED = (
+    AT_XS_TABLE - KIB,
+    AT_WS_RAW - 3 * KIB,
+)
+AT_SEL_RAW = AT_WS_RAW + KIB
+AT_SEL2 = AT_X_TABLE[1]
+AT_W3_WORDS = AT_X_TABLE[1] + 8 * KIB
+AT_W3_SCALES = AT_X_TABLE[1] + 9 * KIB
+AT_W_DEALT = {
+    1: AT_XS_TABLE + 3 * KIB,
+    2: AT_X_TABLE[1] + 12 * KIB,
+    3: AT_X_TABLE[1] + 13 * KIB,
+}
 
 
 def tile_picked_yjoinsz_rel_p_kernel(
@@ -37,257 +59,264 @@ def tile_picked_yjoinsz_rel_p_kernel(
         early = ctx.enter_context(tc.tile_pool(name="early", bufs=1))
         psum = ctx.enter_context(tc.psum_pool(name="psum", bufs=1))
 
-        offs_sb = keep.tile([P, S // 16], U16, name="offs_sb")
-        jn_sb = keep.tile([P, S // 16], U16, name="jn_sb")
-        qry_sb = keep.tile([P, U // 16], U16, name="qry_sb")
+        def entries(list_tile, cols):
+            return list_tile[:, cols.start // PER_COLUMN:cols.stop // PER_COLUMN]
+
+        def key_half(h):
+            return slice(BANK * h, BANK * (h + 1))
+
+        def scale_rows(q):
+            return slice(32 * q, 32 * q + 4)
+
+        offs_sb = keep.tile([P, S // PER_COLUMN], U16, name="offs_sb")
+        jn_sb = keep.tile([P, S // PER_COLUMN], U16, name="jn_sb")
+        qry_sb = keep.tile([P, U // PER_COLUMN], U16, name="qry_sb")
         nc.sync.dma_start(offs_sb[:], offs)
         nc.sync.dma_start(jn_sb[:], jn)
         nc.sync.dma_start(qry_sb[:], qry)
 
+        unit_sb = early.tile([P, PACK], F32, name="unit_sb", align_bytes=64, offset=AT_UNIT)
+        nc.sync.dma_start(unit_sb[:], unit.rearrange("(p t) one -> p (t one)", t=PACK))
+        unit2 = keep.tile([P, PACK], F32, name="unit2")
+        nc.vector.tensor_scalar(unit2[:], unit_sb[:], 2.0, None, ALU.mult)
+
         x_table = []
         for o in range(PASSES):
-            table = early.tile([P, T], I32, name="x_table%d" % o, align_bytes=64, offset=X_TABLE[o])
-            nc.gpsimd.dma_start(table[:], x_words[o].rearrange("p n t -> p (n t)").bitcast(I32))
+            table = early.tile([P, T], I32, name="x_table%d" % o, align_bytes=64, offset=AT_X_TABLE[o])
+            nc.sync.dma_start(table[:], x_words[o].rearrange("p n t -> p (n t)").bitcast(I32))
             x_table.append(table)
 
-        xs_table = early.tile([P, T], U8, name="xs_table", align_bytes=64, offset=XS_TABLE)
+        xs_table = early.tile([P, T], U8, name="xs_table", align_bytes=64, offset=AT_XS_TABLE)
         nc.vector.memset(xs_table[:].bitcast(I32), 0)
-        ws_raw = early.tile([P, 2, PASSES, H], U8, name="ws_raw", align_bytes=64, offset=WS_RAW)
+        ws_raw = early.tile([P, 2, PASSES, H], U8, name="ws_raw", align_bytes=64, offset=AT_WS_RAW)
         nc.vector.memset(ws_raw[:].bitcast(I32), 0)
         w_raw = keep.tile([P, 2, PASSES, 2 * H], U8, name="w_raw", align_bytes=64)
-        for i, words in enumerate((w1_words, w2_words)):
-            nc.scalar.dma_start(w_raw[:, i].bitcast(I32), words.rearrange("o p c -> p o c").bitcast(I32))
+        for rel, words in ((FREQ, w1_words), (FRQ2, w2_words)):
+            nc.scalar.dma_start(w_raw[:, rel].bitcast(I32), words.rearrange("o p c -> p o c").bitcast(I32))
         nc.scalar.dma_start(xs_table[0:32].bitcast(I32), x_scales.rearrange("o q c -> (o q) c").bitcast(I32))
 
-        unit2 = keep.tile([P, D], F32, name="unit2")
         tiny = keep.tile([P, 1], F32, name="tiny")
-        for i, scales in enumerate((w1_scales, w2_scales)):
-            for q in range(4):
-                nc.sync.dma_start(
-                    ws_raw[32 * q:32 * q + 4, i].bitcast(I32),
-                    scales[:, 4 * q:4 * q + 4, :].rearrange("o r c -> r o c").bitcast(I32))
+        for rel, w_scales in ((FREQ, w1_scales), (FRQ2, w2_scales)):
+            for q in range(QUADRANTS):
+                queue = nc.scalar if QUADRANTS * rel + q < SCALE_LOADS_ON_SCALAR else nc.gpsimd
+                queue.dma_start(
+                    ws_raw[scale_rows(q), rel].bitcast(I32),
+                    w_scales[:, 4 * q:4 * q + 4, :].rearrange("o r c -> r o c").bitcast(I32))
         nc.vector.memset(tiny[:], TINY)
 
         w_dealt = [keep.tile([P, 2 * PASSES, P, 2], U8, name="w_dealt0", align_bytes=64)]
-        ws_dealt = early.tile([P, D, 2 * PASSES, P], U8, name="ws_dealt", align_bytes=64, offset=XS_TABLE + 5120)
-        for t in range(1, D):
-            w_dealt.append(early.tile([P, 2 * PASSES, P, 2], U8, name="w_dealt%d" % t, align_bytes=64, offset=XS_TABLE + 3072 if t == 1 else LATE + 10240 + 1024 * t))
+        ws_dealt = keep.tile([P, PACK, 2 * PASSES, P], U8, name="ws_dealt", align_bytes=64)
+        for t in range(1, PACK):
+            w_dealt.append(early.tile(
+                [P, 2 * PASSES, P, 2], U8, name="w_dealt%d" % t, align_bytes=64, offset=AT_W_DEALT[t]))
 
         def deal_words(t):
-            src = w_raw[:].rearrange("p i o (m t b) -> p (i o) t m b", t=D, b=2)
-            nc.vector.tensor_copy(w_dealt[t][:].bitcast(U16), src[:, :, t].bitcast(U16))
+            by_tile = w_raw[:].rearrange("p rel o (m t b) -> p (rel o) t m b", t=PACK, b=2)
+            nc.vector.tensor_copy(w_dealt[t][:].bitcast(U16), by_tile[:, :, t].bitcast(U16))
 
-        def deal_scales(i):
-            nc.vector.tensor_copy(ws_dealt[:, :, PASSES * i:PASSES * (i + 1)].rearrange("p t g m -> p (g m) t"), ws_raw[:, i].rearrange("p o (m t) -> p (o m) t", t=D))
+        def deal_scales(rel):
+            nc.vector.tensor_copy(
+                ws_dealt[:, :, PASSES * rel:PASSES * (rel + 1)].rearrange("p t g m -> p (g m) t"),
+                ws_raw[:, rel].rearrange("p o (m t) -> p (o m) t", t=PACK))
 
-        xg1 = early.tile([P, S], U32, name="xg1", align_bytes=64, offset=0)
-        xg0 = early.tile([P, S], U32, name="xg0", align_bytes=64, offset=XS_TABLE - 1024)
-        xg = [[xg0[:, 0:HALF], xg0[:, HALF:S]],
-              [xg1[:, 0:HALF], xg1[:, HALF:S]]]
+        x_picked = [
+            early.tile([P, S], U32, name="x_picked%d" % o, align_bytes=64, offset=AT_X_PICKED[o])
+            for o in range(PASSES)]
         xs_picked = keep.tile([P, S], U8, name="xs_picked", align_bytes=64)
-        xsg = keep.tile([P, PASSES, S], U8, name="xsg", align_bytes=64)
-
-        nc.vector.memset(xsg[:].bitcast(I32), 0)
+        xs_placed = keep.tile([P, PASSES, S], U8, name="xs_placed", align_bytes=64)
+        nc.vector.memset(xs_placed[:].bitcast(I32), 0)
 
         def gather_scales():
             nc.vector.tensor_copy(xs_picked[:], xs_table[:].indirect(offs_sb[:]))
             for o in range(PASSES):
-                for q in range(4):
+                for q in range(QUADRANTS):
                     row = 16 * o + 4 * q
-                    nc.sync.dma_start(xsg[32 * q:32 * q + 4, o].bitcast(I32), xs_picked[row:row + 4].bitcast(I32))
+                    queue = nc.gpsimd if (o, q) == (PASSES - 1, QUADRANTS - 1) else nc.scalar
+                    queue.dma_start(
+                        xs_placed[scale_rows(q), o].bitcast(I32), xs_picked[row:row + 4].bitcast(I32))
 
         def gather_words(o, h):
-            nc.vector.tensor_copy(xg[o][h][:], x_table[o][:].bitcast(U32).indirect(offs_sb[:, 32 * h:32 * h + 32]))
+            nc.vector.tensor_copy(
+                x_picked[o][:, key_half(h)],
+                x_table[o][:].bitcast(U32).indirect(entries(offs_sb, key_half(h))))
 
         deal_words(0)
         gather_scales()
         deal_words(1)
-        deal_scales(0)
-        deal_scales(1)
         gather_words(0, 0)
         gather_words(0, 1)
+        deal_scales(FREQ)
+        deal_scales(FRQ2)
         gather_words(1, 0)
         gather_words(1, 1)
-        for t in range(2, D):
-            deal_words(t)
-        w3w = early.tile([P, 2 * N], U8, name="w3w", align_bytes=64, offset=LATE + 8192)
-        nc.sync.dma_start(w3w[:].bitcast(I32), w3_words[0].bitcast(I32))
-        unit_sb = early.tile([P, D], F32, name="unit_sb", align_bytes=64, offset=LATE + 8192 + 512)
-        nc.sync.dma_start(unit_sb[:], unit.rearrange("(p t) one -> p (t one)", t=D))
-        w3s = early.tile([P, N], U8, name="w3s", align_bytes=64, offset=LATE + 8192 + 1024)
-        nc.gpsimd.memset(w3s[:].bitcast(I32), 0)
-        for q in range(4):
+        deal_words(2)
+        deal_words(3)
+
+        w3_words_sb = early.tile([P, 2 * N], U8, name="w3_words_sb", align_bytes=64, offset=AT_W3_WORDS)
+        nc.sync.dma_start(w3_words_sb[:].bitcast(I32), w3_words[0].bitcast(I32))
+        w3_scales_sb = early.tile([P, N], U8, name="w3_scales_sb", align_bytes=64, offset=AT_W3_SCALES)
+        nc.gpsimd.memset(w3_scales_sb[:].bitcast(I32), 0)
+        for q in range(QUADRANTS):
             nc.sync.dma_start(
-                w3s[32 * q:32 * q + 4].bitcast(I32), w3_scales[0, 4 * q:4 * q + 4, :].bitcast(I32))
-        nc.gpsimd.tensor_scalar(unit2[:], unit_sb[:], 2.0, 0.0, ALU.mult, ALU.add)
+                w3_scales_sb[scale_rows(q)].bitcast(I32), w3_scales[0, 4 * q:4 * q + 4, :].bitcast(I32))
 
-        sel_sb = early.tile([P, D, U], F32, name="sel_sb", align_bytes=64, offset=LATE)
-        nc.sync.dma_start(sel_sb[:], sel.rearrange("(p t) r -> p t r", t=D))
+        sel2 = early.tile([P, PACK, U], F32, name="sel2", align_bytes=64, offset=AT_SEL2)
+        sel_raw = early.tile([P, PACK, U], F32, name="sel_raw", align_bytes=64, offset=AT_SEL_RAW)
+        nc.sync.dma_start(sel_raw[:], sel.rearrange("(p t) r -> p t r", t=PACK))
+        for t in (1, 0, 2, 3):
+            nc.vector.tensor_scalar(sel2[:, t], sel_raw[:, t], unit2[:, t:t + 1], None, ALU.mult)
 
-        ring = [keep.tile([P, 5 + r, S], F32, name="ring%d" % r) for r in range(2)]
+        work = [keep.tile([P, 5, S], F32, name="work0"), keep.tile([P, 6, S], F32, name="work1")]
         banks = {}
-
-        def product(kind, t, h, slot, passes=range(PASSES)):
-            if 0 in passes:
-                banks[kind, t, h] = psum.tile([P, HALF], F32, name="acc", tag="bank%d" % (2 * slot + h))
-            acc = banks[kind, t, h]
-            for o in passes:
-                g = PASSES * kind + o
-                nc.tensor.matmul_mx(
-                    out=acc[:],
-                    lhsT=w_dealt[t][:, g].rearrange("p m b -> p (m b)").bitcast(FP4X4),
-                    lhsT_scale=ws_dealt[:, t, g],
-                    rhs=xg[o][h][:].bitcast(FP8X4),
-                    rhs_scale=xsg[:, o, HALF * h:HALF * (h + 1)],
-                    start=(o == 0), stop=(o == PASSES - 1))
-
         place = {}
 
-        def sigmoid(kind, t, h):
-            r, i = place[kind, t]
-            nc.scalar.activation(ring[r][:, i + 1 + r, HALF * h:HALF * (h + 1)], banks[kind, t, h][:], ACT.Sigmoid, scale=-1.0)
+        def product(rel, t, h, slot, passes):
+            opens, closes = h, 1 - h
+            if opens in passes:
+                banks[rel, t, h] = psum.tile([P, BANK], F32, name="acc", tag="bank%d" % (2 * slot + h))
+            for o in passes:
+                g = PASSES * rel + o
+                nc.tensor.matmul_mx(
+                    out=banks[rel, t, h][:],
+                    lhsT=w_dealt[t][:, g].rearrange("p m b -> p (m b)").bitcast(FP4X4),
+                    lhsT_scale=ws_dealt[:, t, g],
+                    rhs=x_picked[o][:, key_half(h)].bitcast(FP8X4),
+                    rhs_scale=xs_placed[:, o, key_half(h)],
+                    start=(o == opens), stop=(o == closes))
 
-        def log(kind, t):
-            r, i = place[kind, t]
-            nc.scalar.activation(ring[r][:, i], ring[r][:, i + 1], ACT.Ln, bias=tiny[:])
+        def sigmoid(rel, t, h):
+            r, i = place[rel, t]
+            nc.scalar.activation(
+                work[r][:, i + 1 + r, key_half(h)], banks[rel, t, h][:], ACT.Sigmoid, scale=-1.0)
 
-        def log_pair(r, i):
-            nc.scalar.activation(ring[r][:, i:i + 2], ring[r][:, i + 2:i + 4], ACT.Ln, bias=tiny[:])
+        def log(dst, src):
+            nc.scalar.activation(dst, src, ACT.Ln, bias=tiny[:])
 
-        soft = {}
+        soft = {
+            (rel, t): keep.tile([P, S], F32, name="soft%d_%d" % (rel, t))
+            for rel in (FREQ, FRQ2) for t in range(PACK)}
 
-        for kind in range(2):
-            for t in range(D):
-                soft[kind, t] = keep.tile([P, S], F32, name="soft%d_%d" % (kind, t))
+        def softplus(rel, t, h):
+            r, i = place[rel, t]
+            nc.vector.scalar_tensor_tensor(
+                soft[rel, t][:, key_half(h)], work[r][:, i, key_half(h)], -1.0, banks[rel, t, h][:],
+                ALU.mult, ALU.max)
 
-        def softplus(kind, t, h):
-            r, i = place[kind, t]
-            cols = slice(HALF * h, HALF * (h + 1))
-            nc.vector.scalar_tensor_tensor(soft[kind, t][:, cols], ring[r][:, i, cols], -1.0, banks[kind, t, h][:], ALU.mult, ALU.max)
-
-        recip_w = [keep.tile([P, WINDOW], F32, name="recip_w%d" % t) for t in range(D)]
-        ratio_w = [keep.tile([P, WINDOW], F32, name="ratio_w%d" % t) for t in range(D)]
+        recip_window = [keep.tile([P, WINDOW], F32, name="recip_window%d" % t) for t in range(PACK)]
+        size_window = [keep.tile([P, WINDOW], F32, name="size_window%d" % t) for t in range(PACK)]
         heavy_late = keep.tile([P, 8, 64], F32, name="heavy_late")
-        heavy = [ring[1][:, 2:6].rearrange("p a (h c) -> p (a h) c", h=2)[:, :, 0:64], heavy_late[:]]
+        heavy = [work[1][:, 2:6].rearrange("p a (h c) -> p (a h) c", h=2)[:, :, 0:64], heavy_late[:]]
         log_heavy = [keep.tile([P, 2 * V], F32, name="log_heavy%d" % r) for r in range(2)]
 
         def pair_largest(t):
-            f = soft[0, t]
-            nc.vector.tensor_tensor(recip_w[t][:, V:], f[:, 0::2], f[:, 1::2], ALU.max)
+            freq = soft[FREQ, t]
+            nc.vector.tensor_tensor(recip_window[t][:, V:], freq[:, 0::2], freq[:, 1::2], ALU.max)
 
-        def largest(t):
-            pairs = recip_w[t][:, V:]
-            pv = pairs.rearrange("p (a c e) -> p e a c", a=4, e=2)
-            dst = heavy[t // 2][:, 4 * (t % 2):4 * (t % 2) + 4]
-            nc.vector.scalar_tensor_tensor(dst, pv[:, 0], 0.0, pv[:, 1], ALU.max, ALU.max)
+        def group_largest(t):
+            pairs = recip_window[t][:, V:].rearrange("p (a c e) -> p e a c", a=4, e=2)
+            pieces = heavy[t // 2][:, 4 * (t % 2):4 * (t % 2) + 4]
+            nc.vector.scalar_tensor_tensor(pieces, pairs[:, 0], 0.0, pairs[:, 1], ALU.max, ALU.max)
 
         def log_of_heavy(r):
-            nc.scalar.activation(log_heavy[r][:].rearrange("p (a c) -> p a c", a=8), heavy[r], ACT.Ln, bias=tiny[:], scale=2.0)
+            nc.scalar.activation(
+                log_heavy[r][:].rearrange("p (a c) -> p a c", a=8), heavy[r], ACT.Ln, bias=tiny[:], scale=2.0)
 
         def reciprocal(t):
             cols = slice(V * (t % 2), V * (t % 2 + 1))
-            nc.scalar.activation(recip_w[t][:, 0:V], log_heavy[t // 2][:, cols], ACT.Sigmoid, scale=-1.0)
+            nc.scalar.activation(recip_window[t][:, 0:V], log_heavy[t // 2][:, cols], ACT.Sigmoid, scale=-1.0)
 
-        match = [keep.tile([P, S], F32, name="match%d" % t) for t in range(D)]
+        def softplus_and_pairs(a, b):
+            softplus(FREQ, a, 1)
+            softplus(FREQ, a, 0)
+            softplus(FREQ, b, 0)
+            pair_largest(a)
+            softplus(FREQ, b, 1)
+            group_largest(a)
+            pair_largest(b)
+
+        match = [keep.tile([P, S], F32, name="match%d" % t) for t in range(PACK)]
+        partner = {t: keep.tile([P, S], F32, name="partner%d" % t) for t in (2, 3)}
 
         def match_fused(t, h):
-            cols = slice(HALF * h, HALF * (h + 1))
-            nc.vector.tensor_tensor(match[t][:, cols], soft[1, t][:].indirect(jn_sb[:, 32 * h:32 * h + 32]), soft[0, t][:, cols], ALU.mult)
-
-        partner = {}
+            cols = key_half(h)
+            nc.vector.tensor_tensor(
+                match[t][:, cols], soft[FRQ2, t][:].indirect(entries(jn_sb, cols)), soft[FREQ, t][:, cols], ALU.mult)
 
         def fetch_partner(t):
-            tile = keep.tile([P, S], F32, name="partner%d" % t)
             for h in range(2):
-                cols = slice(HALF * h, HALF * (h + 1))
-                nc.scalar.activation(tile[:, cols], soft[1, t][:].indirect(jn_sb[:, 32 * h:32 * h + 32]), ACT.Copy)
-            partner[t] = tile
+                cols = key_half(h)
+                nc.scalar.activation(partner[t][:, cols], soft[FRQ2, t][:].indirect(entries(jn_sb, cols)), ACT.Copy)
 
         def match_plain(t):
-            nc.vector.tensor_tensor(match[t][:], partner[t][:], soft[0, t][:], ALU.mult)
+            nc.vector.tensor_tensor(match[t][:], partner[t][:], soft[FREQ, t][:], ALU.mult)
 
         def pair_sum(t):
-            nc.vector.tensor_tensor(ratio_w[t][:, V:], match[t][:, 0::2], match[t][:, 1::2], ALU.add)
+            nc.vector.tensor_tensor(size_window[t][:, V:], match[t][:, 0::2], match[t][:, 1::2], ALU.add)
 
         def group_sum(t):
-            pairs = ratio_w[t][:, V:]
-            nc.vector.tensor_tensor(sizes[:, t], pairs[:, 0::2], pairs[:, 1::2], ALU.add)
+            pairs = size_window[t][:, V:]
+            nc.vector.tensor_tensor(size_window[t][:, 0:V], pairs[:, 0::2], pairs[:, 1::2], ALU.add)
 
-        def ratio(t):
-            nc.vector.scalar_tensor_tensor(ratio_w[t][:, 0:V], sizes[:, t], unit2[:, t:t + 1], recip_w[t][:, 0:V], ALU.mult, ALU.mult)
-
-        term_rest = keep.tile([P, D, U], F32, name="term_rest")
-        term = [ring[1][:, 3, HALF:S], term_rest[:, 1], term_rest[:, 2], term_rest[:, 3]]
+        term = keep.tile([P, PACK, U], F32, name="term")
         recip_late = keep.tile([P, 2, U], F32, name="recip_late")
-        recip_q = [ring[1][:, 5, 0:U], ring[1][:, 5, U:2 * U], recip_late[:, 0], recip_late[:, 1]]
-        hid = keep.tile([P, D, U], F32, name="hid")
-        sizes = keep.tile([P, D, V], F32, name="sizes")
+        recip_q = [work[1][:, 5, 0:U], work[1][:, 5, U:2 * U], recip_late[:, 0], recip_late[:, 1]]
+        hid = keep.tile([P, PACK, U], F32, name="hid")
+        grouped = [keep.tile([P, HALF_U, PACK], BF16, name="grouped%d" % h, align_bytes=64) for h in range(2)]
+        all_queries = slice(0, U)
+        query_half = [slice(0, HALF_U), slice(HALF_U, U)]
 
-        ratio_late = keep.tile([P, 2, U], F32, name="ratio_late")
-        ratio_q = [ring[1][:, 4, 0:U], ring[1][:, 4, U:2 * U], ratio_late[:, 0], ratio_late[:, 1]]
+        def size_times_sel(t, cols):
+            nc.vector.tensor_tensor(
+                term[:, t, cols], size_window[t][:].indirect(entries(qry_sb, cols)), sel2[:, t, cols], ALU.mult)
 
-        def ratio_times_sel(t, a=0, b=U):
-            nc.vector.tensor_tensor(term[t][:, a:b], ratio_w[t][:].indirect(qry_sb[:, a // 16:b // 16]), sel_sb[:, t, a:b], ALU.mult)
+        def fetch_recip(t, cols):
+            nc.scalar.activation(recip_q[t][:, cols], recip_window[t][:].indirect(entries(qry_sb, cols)), ACT.Copy)
 
-        def fetch_recip(t, a=0, b=U):
-            nc.scalar.activation(recip_q[t][:, a:b], recip_w[t][:].indirect(qry_sb[:, a // 16:b // 16]), ACT.Copy)
-
-        def hidden(t, a=0, b=U):
-            nc.vector.scalar_tensor_tensor(hid[:, t, a:b], recip_q[t][:, a:b], unit2[:, t:t + 1], term[t][:, a:b], ALU.mult, ALU.add)
-
-        def fetch_ratio(t, a=0, b=U):
-            nc.scalar.activation(ratio_q[t][:, a:b], ratio_w[t][:].indirect(qry_sb[:, a // 16:b // 16]), ACT.Copy)
-
-        def fetched_times_sel(t, a=0, b=U):
-            nc.vector.tensor_tensor(term[t][:, a:b], ratio_q[t][:, a:b], sel_sb[:, t, a:b], ALU.mult)
-
-        R = U // 2
-        grouped = [keep.tile([P, R, D], BF16, name="grouped%d" % h, align_bytes=64) for h in range(2)]
+        def hidden(t, cols):
+            nc.vector.scalar_tensor_tensor(
+                hid[:, t, cols], term[:, t, cols], unit2[:, t:t + 1], recip_q[t][:, cols], ALU.add, ALU.mult)
 
         def interleave(h):
             copy = nc.scalar.copy if h == 0 else nc.vector.tensor_copy
             copy(grouped[h][:].rearrange("p (c i) t -> p c t i", i=4),
-                 hid[:, :, R * h:R * (h + 1)].rearrange("p t (c i) -> p c t i", i=4))
+                 hid[:, :, query_half[h]].rearrange("p t (c i) -> p c t i", i=4))
 
-        logs = [(0, 1), (0, 0), (1, 1), (1, 0)]
-        for i, key in enumerate(logs):
+        order = [(FREQ, 1), (FREQ, 0), (FRQ2, 1), (FRQ2, 0)]
+        for i, key in enumerate(order):
             place[key] = (0, i)
-        for kind, t in logs:
-            product(kind, t, 0, place[kind, t][1], [0])
-        for kind, t in logs:
-            product(kind, t, 0, place[kind, t][1], [1])
-            sigmoid(kind, t, 0)
-        for kind, t in reversed(logs):
-            product(kind, t, 1, place[kind, t][1])
-            sigmoid(kind, t, 1)
-        for kind, t in logs:
-            log(kind, t)
-        def softplus_and_largest(a, b):
-            softplus(0, a, 0)
-            softplus(0, a, 1)
-            softplus(0, b, 0)
-            pair_largest(a)
-            softplus(0, b, 1)
-            largest(a)
-            pair_largest(b)
-
-        softplus_and_largest(1, 0)
-        softplus(1, 1, 0)
-        largest(0)
-        softplus(1, 1, 1)
-        softplus(1, 0, 0)
-        softplus(1, 0, 1)
+        first_last = order[1:] + order[:1]
+        for rel, t in order:
+            product(rel, t, 0, place[rel, t][1], (0,))
+        for rel, t in first_last:
+            product(rel, t, 0, place[rel, t][1], (1,))
+        for rel, t in first_last:
+            product(rel, t, 1, place[rel, t][1], (1, 0))
+        for h in range(2):
+            for rel, t in order[1:]:
+                sigmoid(rel, t, h)
+        for h in range(2):
+            sigmoid(*order[0], h)
+        for h in (1, 0):
+            log(work[0][:, 0, key_half(h)], work[0][:, 1, key_half(h)])
+        for i in range(1, len(order)):
+            log(work[0][:, i], work[0][:, i + 1])
+        softplus_and_pairs(1, 0)
+        softplus(FRQ2, 1, 0)
+        group_largest(0)
+        softplus(FRQ2, 1, 1)
+        softplus(FRQ2, 0, 0)
+        softplus(FRQ2, 0, 1)
         log_of_heavy(0)
         reciprocal(1)
         reciprocal(0)
 
-        logs = [(1, 2), (1, 3), (0, 2), (0, 3)]
-        for i, key in enumerate(logs):
+        order = [(FRQ2, 2), (FRQ2, 3), (FREQ, 2), (FREQ, 3)]
+        for i, key in enumerate(order):
             place[key] = (1, i)
-        for slot, (kind, t) in enumerate(logs[2:] + logs[:2]):
+        for slot, (rel, t) in enumerate(order[2:] + order[:2]):
             for h in range(2):
-                product(kind, t, h, slot)
-                sigmoid(kind, t, h)
+                product(rel, t, h, slot, (h, 1 - h))
+                sigmoid(rel, t, h)
         match_fused(1, 0)
         match_fused(1, 1)
         match_fused(0, 0)
@@ -295,61 +324,55 @@ def tile_picked_yjoinsz_rel_p_kernel(
         match_fused(0, 1)
         group_sum(1)
         pair_sum(0)
-        ratio(1)
         group_sum(0)
-        ratio_times_sel(1)
-        ratio(0)
-        log_pair(1, 0)
-        log_pair(1, 2)
+        size_times_sel(1, all_queries)
+        size_times_sel(0, all_queries)
+        for i in (0, 2):
+            log(work[1][:, i:i + 2], work[1][:, i + 2:i + 4])
         for t in (2, 3):
             for h in range(2):
-                softplus(1, t, h)
+                softplus(FRQ2, t, h)
         fetch_partner(2)
         fetch_partner(3)
-        softplus_and_largest(2, 3)
-        ratio_times_sel(0)
-        largest(3)
+        softplus_and_pairs(2, 3)
+        match_plain(2)
+        group_largest(3)
         log_of_heavy(1)
         reciprocal(2)
         reciprocal(3)
         for t in (1, 0):
-            fetch_recip(t)
-        for a in (0, 256):
+            fetch_recip(t, all_queries)
+        for cols in query_half:
             for t in (2, 3):
-                fetch_recip(t, a, a + 256)
-        match_plain(2)
+                fetch_recip(t, cols)
         match_plain(3)
         pair_sum(2)
         pair_sum(3)
         group_sum(2)
         group_sum(3)
-        hidden(1)
-        ratio(3)
-        ratio(2)
-        hidden(0)
-        for a in (0, 256):
-            if a:
-                fetch_ratio(3, a, a + 256)
-                fetched_times_sel(3, a, a + 256)
-            else:
-                ratio_times_sel(3, a, a + 256)
-            ratio_times_sel(2, a, a + 256)
-            hidden(3, a, a + 256)
-            hidden(2, a, a + 256)
-            interleave(a // 256)
+        hidden(1, all_queries)
+        hidden(0, all_queries)
+        for h, cols in enumerate(query_half):
+            size_times_sel(3, cols)
+            size_times_sel(2, cols)
+            hidden(3, cols)
+            hidden(2, cols)
+            interleave(h)
 
-        for h in range(2):
-            codes = keep.tile([P, R], U32, name="codes%d" % h, align_bytes=64)
-            scales = keep.tile([P, R], U8, name="scales%d" % h, align_bytes=64)
-            nc.vector.quantize_mx(out=codes[:].bitcast(FP8X4), scales=scales[:], in_=grouped[h][:].rearrange("p r t -> p (r t)"))
-            for m in range(N // P):
-                acc = psum.tile([P, HALF], F32, name="acc", tag="bank%d" % (2 * h + m))
+        blocks = N // P
+        for h, cols in enumerate(query_half):
+            codes = keep.tile([P, HALF_U], U32, name="codes%d" % h, align_bytes=64)
+            hid_scales = keep.tile([P, HALF_U], U8, name="hid_scales%d" % h, align_bytes=64)
+            nc.vector.quantize_mx(
+                out=codes[:].bitcast(FP8X4), scales=hid_scales[:], in_=grouped[h][:].rearrange("p r t -> p (r t)"))
+            for m in range(blocks):
+                acc = psum.tile([P, BANK], F32, name="acc", tag="bank%d" % (blocks * h + m))
                 nc.tensor.matmul_mx(
-                    out=acc[:, 0:R],
-                    lhsT=w3w[:, 2 * P * m:2 * P * (m + 1)].bitcast(FP4X4),
-                    lhsT_scale=w3s[:, P * m:P * (m + 1)],
-                    rhs=codes[:].bitcast(FP8X4), rhs_scale=scales[:], start=True, stop=True)
-                res = keep.tile([P, R], F32, name="res%d_%d" % (h, m))
-                copy = nc.vector.tensor_copy if (h, m) == (1, 1) else nc.scalar.copy
-                copy(res[:], acc[:, 0:R])
-                nc.sync.dma_start(out[P * m:P * (m + 1), R * h:R * (h + 1)], res[:])
+                    out=acc[:, 0:HALF_U],
+                    lhsT=w3_words_sb[:, 2 * P * m:2 * P * (m + 1)].bitcast(FP4X4),
+                    lhsT_scale=w3_scales_sb[:, P * m:P * (m + 1)],
+                    rhs=codes[:].bitcast(FP8X4), rhs_scale=hid_scales[:], start=True, stop=True)
+                result = keep.tile([P, HALF_U], F32, name="result%d_%d" % (h, m))
+                copy = nc.vector.tensor_copy if (h, m) == (1, blocks - 1) else nc.scalar.copy
+                copy(result[:], acc[:, 0:HALF_U])
+                nc.sync.dma_start(out[P * m:P * (m + 1), cols], result[:])

from contextlib import ExitStack

import concourse.mybir as mybir

K, T, S, N, H, V, U = 1024, 4096, 1024, 256, 512, 256, 512
FLOPS = 2 * (2 * K * H * S + H * N * U)

F32 = mybir.dt.float32
BF16 = mybir.dt.bfloat16
I32 = mybir.dt.int32
U32 = mybir.dt.uint32
U16 = mybir.dt.uint16
U8 = mybir.dt.uint8
FP8X4 = mybir.dt.float8_e4m3fn_x4
FP4X4 = mybir.dt.float4_e2m1fn_x4
ACT = mybir.ActivationFunctionType
ALU = mybir.AluOpType

P = 128
PACK = 4
PASSES = K // (P * PACK)
QUADRANTS = 4
BANK = 512
PER_COLUMN = 16
HALF_U = U // 2
WINDOW = V + S // 2
TINY = 2.0 ** -60
FREQ, FRQ2 = 0, 1

SCALE_LOADS_ON_SCALAR = 5

KIB = 1024
AT_X_TABLE = (0, 16 * KIB)
AT_WS_RAW = 35 * KIB
AT_XS_TABLE = 45 * KIB
AT_UNIT = AT_X_TABLE[1]
AT_X_PICKED = (
    AT_XS_TABLE - KIB,
    AT_WS_RAW - 3 * KIB,
)
AT_SEL_RAW = AT_WS_RAW + KIB
AT_SEL2 = AT_X_TABLE[1]
AT_W3_WORDS = AT_X_TABLE[1] + 8 * KIB
AT_W3_SCALES = AT_X_TABLE[1] + 9 * KIB
AT_W_DEALT = {
    1: AT_XS_TABLE + 3 * KIB,
    2: AT_X_TABLE[1] + 12 * KIB,
    3: AT_X_TABLE[1] + 13 * KIB,
}


def tile_picked_yjoinsz_rel_p_kernel(
    tc, x_words, x_scales, w1_words, w1_scales, w2_words, w2_scales, sel, unit,
    w3_words, w3_scales, offs, jn, qry, out,
):
    nc = tc.nc
    with ExitStack() as ctx:
        keep = ctx.enter_context(tc.tile_pool(name="keep", bufs=1))
        early = ctx.enter_context(tc.tile_pool(name="early", bufs=1))
        psum = ctx.enter_context(tc.psum_pool(name="psum", bufs=1))

        def entries(list_tile, cols):
            return list_tile[:, cols.start // PER_COLUMN:cols.stop // PER_COLUMN]

        def key_half(h):
            return slice(BANK * h, BANK * (h + 1))

        def scale_rows(q):
            return slice(32 * q, 32 * q + 4)

        offs_sb = keep.tile([P, S // PER_COLUMN], U16, name="offs_sb")
        jn_sb = keep.tile([P, S // PER_COLUMN], U16, name="jn_sb")
        qry_sb = keep.tile([P, U // PER_COLUMN], U16, name="qry_sb")
        nc.sync.dma_start(offs_sb[:], offs)
        nc.sync.dma_start(jn_sb[:], jn)
        nc.sync.dma_start(qry_sb[:], qry)

        unit_sb = early.tile([P, PACK], F32, name="unit_sb", align_bytes=64, offset=AT_UNIT)
        nc.sync.dma_start(unit_sb[:], unit.rearrange("(p t) one -> p (t one)", t=PACK))
        unit2 = keep.tile([P, PACK], F32, name="unit2")
        nc.vector.tensor_scalar(unit2[:], unit_sb[:], 2.0, None, ALU.mult)

        x_table = []
        for o in range(PASSES):
            table = early.tile([P, T], I32, name="x_table%d" % o, align_bytes=64, offset=AT_X_TABLE[o])
            nc.sync.dma_start(table[:], x_words[o].rearrange("p n t -> p (n t)").bitcast(I32))
            x_table.append(table)

        xs_table = early.tile([P, T], U8, name="xs_table", align_bytes=64, offset=AT_XS_TABLE)
        nc.vector.memset(xs_table[:].bitcast(I32), 0)
        ws_raw = early.tile([P, 2, PASSES, H], U8, name="ws_raw", align_bytes=64, offset=AT_WS_RAW)
        nc.vector.memset(ws_raw[:].bitcast(I32), 0)
        w_raw = keep.tile([P, 2, PASSES, 2 * H], U8, name="w_raw", align_bytes=64)
        for rel, words in ((FREQ, w1_words), (FRQ2, w2_words)):
            nc.scalar.dma_start(w_raw[:, rel].bitcast(I32), words.rearrange("o p c -> p o c").bitcast(I32))
        nc.scalar.dma_start(xs_table[0:32].bitcast(I32), x_scales.rearrange("o q c -> (o q) c").bitcast(I32))

        tiny = keep.tile([P, 1], F32, name="tiny")
        for rel, w_scales in ((FREQ, w1_scales), (FRQ2, w2_scales)):
            for q in range(QUADRANTS):
                queue = nc.scalar if QUADRANTS * rel + q < SCALE_LOADS_ON_SCALAR else nc.gpsimd
                queue.dma_start(
                    ws_raw[scale_rows(q), rel].bitcast(I32),
                    w_scales[:, 4 * q:4 * q + 4, :].rearrange("o r c -> r o c").bitcast(I32))
        nc.vector.memset(tiny[:], TINY)

        w_dealt = [keep.tile([P, 2 * PASSES, P, 2], U8, name="w_dealt0", align_bytes=64)]
        ws_dealt = keep.tile([P, PACK, 2 * PASSES, P], U8, name="ws_dealt", align_bytes=64)
        for t in range(1, PACK):
            w_dealt.append(early.tile(
                [P, 2 * PASSES, P, 2], U8, name="w_dealt%d" % t, align_bytes=64, offset=AT_W_DEALT[t]))

        def deal_words(t):
            by_tile = w_raw[:].rearrange("p rel o (m t b) -> p (rel o) t m b", t=PACK, b=2)
            nc.vector.tensor_copy(w_dealt[t][:].bitcast(U16), by_tile[:, :, t].bitcast(U16))

        def deal_scales(rel):
            nc.vector.tensor_copy(
                ws_dealt[:, :, PASSES * rel:PASSES * (rel + 1)].rearrange("p t g m -> p (g m) t"),
                ws_raw[:, rel].rearrange("p o (m t) -> p (o m) t", t=PACK))

        x_picked = [
            early.tile([P, S], U32, name="x_picked%d" % o, align_bytes=64, offset=AT_X_PICKED[o])
            for o in range(PASSES)]
        xs_picked = keep.tile([P, S], U8, name="xs_picked", align_bytes=64)
        xs_placed = keep.tile([P, PASSES, S], U8, name="xs_placed", align_bytes=64)
        nc.vector.memset(xs_placed[:].bitcast(I32), 0)

        def gather_scales():
            nc.vector.tensor_copy(xs_picked[:], xs_table[:].indirect(offs_sb[:]))
            for o in range(PASSES):
                for q in range(QUADRANTS):
                    row = 16 * o + 4 * q
                    queue = nc.gpsimd if (o, q) == (PASSES - 1, QUADRANTS - 1) else nc.scalar
                    queue.dma_start(
                        xs_placed[scale_rows(q), o].bitcast(I32), xs_picked[row:row + 4].bitcast(I32))

        def gather_words(o, h):
            nc.vector.tensor_copy(
                x_picked[o][:, key_half(h)],
                x_table[o][:].bitcast(U32).indirect(entries(offs_sb, key_half(h))))

        deal_words(0)
        gather_scales()
        deal_words(1)
        gather_words(0, 0)
        gather_words(0, 1)
        deal_scales(FREQ)
        deal_scales(FRQ2)
        gather_words(1, 0)
        gather_words(1, 1)
        deal_words(2)
        deal_words(3)

        w3_words_sb = early.tile([P, 2 * N], U8, name="w3_words_sb", align_bytes=64, offset=AT_W3_WORDS)
        nc.sync.dma_start(w3_words_sb[:].bitcast(I32), w3_words[0].bitcast(I32))
        w3_scales_sb = early.tile([P, N], U8, name="w3_scales_sb", align_bytes=64, offset=AT_W3_SCALES)
        nc.gpsimd.memset(w3_scales_sb[:].bitcast(I32), 0)
        for q in range(QUADRANTS):
            nc.sync.dma_start(
                w3_scales_sb[scale_rows(q)].bitcast(I32), w3_scales[0, 4 * q:4 * q + 4, :].bitcast(I32))

        sel2 = early.tile([P, PACK, U], F32, name="sel2", align_bytes=64, offset=AT_SEL2)
        sel_raw = early.tile([P, PACK, U], F32, name="sel_raw", align_bytes=64, offset=AT_SEL_RAW)
        nc.sync.dma_start(sel_raw[:], sel.rearrange("(p t) r -> p t r", t=PACK))
        for t in (1, 0, 2, 3):
            nc.vector.tensor_scalar(sel2[:, t], sel_raw[:, t], unit2[:, t:t + 1], None, ALU.mult)

        work = [keep.tile([P, 5, S], F32, name="work0"), keep.tile([P, 6, S], F32, name="work1")]
        banks = {}
        place = {}

        def product(rel, t, h, slot, passes):
            opens, closes = h, 1 - h
            if opens in passes:
                banks[rel, t, h] = psum.tile([P, BANK], F32, name="acc", tag="bank%d" % (2 * slot + h))
            for o in passes:
                g = PASSES * rel + o
                nc.tensor.matmul_mx(
                    out=banks[rel, t, h][:],
                    lhsT=w_dealt[t][:, g].rearrange("p m b -> p (m b)").bitcast(FP4X4),
                    lhsT_scale=ws_dealt[:, t, g],
                    rhs=x_picked[o][:, key_half(h)].bitcast(FP8X4),
                    rhs_scale=xs_placed[:, o, key_half(h)],
                    start=(o == opens), stop=(o == closes))

        def sigmoid(rel, t, h):
            r, i = place[rel, t]
            nc.scalar.activation(
                work[r][:, i + 1 + r, key_half(h)], banks[rel, t, h][:], ACT.Sigmoid, scale=-1.0)

        def log(dst, src):
            nc.scalar.activation(dst, src, ACT.Ln, bias=tiny[:])

        soft = {
            (rel, t): keep.tile([P, S], F32, name="soft%d_%d" % (rel, t))
            for rel in (FREQ, FRQ2) for t in range(PACK)}

        def softplus(rel, t, h):
            r, i = place[rel, t]
            nc.vector.scalar_tensor_tensor(
                soft[rel, t][:, key_half(h)], work[r][:, i, key_half(h)], -1.0, banks[rel, t, h][:],
                ALU.mult, ALU.max)

        recip_window = [keep.tile([P, WINDOW], F32, name="recip_window%d" % t) for t in range(PACK)]
        size_window = [keep.tile([P, WINDOW], F32, name="size_window%d" % t) for t in range(PACK)]
        heavy_late = keep.tile([P, 8, 64], F32, name="heavy_late")
        heavy = [work[1][:, 2:6].rearrange("p a (h c) -> p (a h) c", h=2)[:, :, 0:64], heavy_late[:]]
        log_heavy = [keep.tile([P, 2 * V], F32, name="log_heavy%d" % r) for r in range(2)]

        def pair_largest(t):
            freq = soft[FREQ, t]
            nc.vector.tensor_tensor(recip_window[t][:, V:], freq[:, 0::2], freq[:, 1::2], ALU.max)

        def group_largest(t):
            pairs = recip_window[t][:, V:].rearrange("p (a c e) -> p e a c", a=4, e=2)
            pieces = heavy[t // 2][:, 4 * (t % 2):4 * (t % 2) + 4]
            nc.vector.scalar_tensor_tensor(pieces, pairs[:, 0], 0.0, pairs[:, 1], ALU.max, ALU.max)

        def log_of_heavy(r):
            nc.scalar.activation(
                log_heavy[r][:].rearrange("p (a c) -> p a c", a=8), heavy[r], ACT.Ln, bias=tiny[:], scale=2.0)

        def reciprocal(t):
            cols = slice(V * (t % 2), V * (t % 2 + 1))
            nc.scalar.activation(recip_window[t][:, 0:V], log_heavy[t // 2][:, cols], ACT.Sigmoid, scale=-1.0)

        def softplus_and_pairs(a, b):
            softplus(FREQ, a, 1)
            softplus(FREQ, a, 0)
            softplus(FREQ, b, 0)
            pair_largest(a)
            softplus(FREQ, b, 1)
            group_largest(a)
            pair_largest(b)

        match = [keep.tile([P, S], F32, name="match%d" % t) for t in range(PACK)]
        partner = {t: keep.tile([P, S], F32, name="partner%d" % t) for t in (2, 3)}

        def match_fused(t, h):
            cols = key_half(h)
            nc.vector.tensor_tensor(
                match[t][:, cols], soft[FRQ2, t][:].indirect(entries(jn_sb, cols)), soft[FREQ, t][:, cols], ALU.mult)

        def fetch_partner(t):
            for h in range(2):
                cols = key_half(h)
                nc.scalar.activation(partner[t][:, cols], soft[FRQ2, t][:].indirect(entries(jn_sb, cols)), ACT.Copy)

        def match_plain(t):
            nc.vector.tensor_tensor(match[t][:], partner[t][:], soft[FREQ, t][:], ALU.mult)

        def pair_sum(t):
            nc.vector.tensor_tensor(size_window[t][:, V:], match[t][:, 0::2], match[t][:, 1::2], ALU.add)

        def group_sum(t):
            pairs = size_window[t][:, V:]
            nc.vector.tensor_tensor(size_window[t][:, 0:V], pairs[:, 0::2], pairs[:, 1::2], ALU.add)

        term = keep.tile([P, PACK, U], F32, name="term")
        recip_late = keep.tile([P, 2, U], F32, name="recip_late")
        recip_q = [work[1][:, 5, 0:U], work[1][:, 5, U:2 * U], recip_late[:, 0], recip_late[:, 1]]
        hid = keep.tile([P, PACK, U], F32, name="hid")
        grouped = [keep.tile([P, HALF_U, PACK], BF16, name="grouped%d" % h, align_bytes=64) for h in range(2)]
        all_queries = slice(0, U)
        query_half = [slice(0, HALF_U), slice(HALF_U, U)]

        def size_times_sel(t, cols):
            nc.vector.tensor_tensor(
                term[:, t, cols], size_window[t][:].indirect(entries(qry_sb, cols)), sel2[:, t, cols], ALU.mult)

        def fetch_recip(t, cols):
            nc.scalar.activation(recip_q[t][:, cols], recip_window[t][:].indirect(entries(qry_sb, cols)), ACT.Copy)

        def hidden(t, cols):
            nc.vector.scalar_tensor_tensor(
                hid[:, t, cols], term[:, t, cols], unit2[:, t:t + 1], recip_q[t][:, cols], ALU.add, ALU.mult)

        def interleave(h):
            copy = nc.scalar.copy if h == 0 else nc.vector.tensor_copy
            copy(grouped[h][:].rearrange("p (c i) t -> p c t i", i=4),
                 hid[:, :, query_half[h]].rearrange("p t (c i) -> p c t i", i=4))

        order = [(FREQ, 1), (FREQ, 0), (FRQ2, 1), (FRQ2, 0)]
        for i, key in enumerate(order):
            place[key] = (0, i)
        first_last = order[1:] + order[:1]
        for rel, t in order:
            product(rel, t, 0, place[rel, t][1], (0,))
        for rel, t in first_last:
            product(rel, t, 0, place[rel, t][1], (1,))
        for rel, t in first_last:
            product(rel, t, 1, place[rel, t][1], (1, 0))
        for h in range(2):
            for rel, t in order[1:]:
                sigmoid(rel, t, h)
        for h in range(2):
            sigmoid(*order[0], h)
        for h in (1, 0):
            log(work[0][:, 0, key_half(h)], work[0][:, 1, key_half(h)])
        for i in range(1, len(order)):
            log(work[0][:, i], work[0][:, i + 1])
        softplus_and_pairs(1, 0)
        softplus(FRQ2, 1, 0)
        group_largest(0)
        softplus(FRQ2, 1, 1)
        softplus(FRQ2, 0, 0)
        softplus(FRQ2, 0, 1)
        log_of_heavy(0)
        reciprocal(1)
        reciprocal(0)

        order = [(FRQ2, 2), (FRQ2, 3), (FREQ, 2), (FREQ, 3)]
        for i, key in enumerate(order):
            place[key] = (1, i)
        for slot, (rel, t) in enumerate(order[2:] + order[:2]):
            for h in range(2):
                product(rel, t, h, slot, (h, 1 - h))
                sigmoid(rel, t, h)
        match_fused(1, 0)
        match_fused(1, 1)
        match_fused(0, 0)
        pair_sum(1)
        match_fused(0, 1)
        group_sum(1)
        pair_sum(0)
        group_sum(0)
        size_times_sel(1, all_queries)
        size_times_sel(0, all_queries)
        for i in (0, 2):
            log(work[1][:, i:i + 2], work[1][:, i + 2:i + 4])
        for t in (2, 3):
            for h in range(2):
                softplus(FRQ2, t, h)
        fetch_partner(2)
        fetch_partner(3)
        softplus_and_pairs(2, 3)
        match_plain(2)
        group_largest(3)
        log_of_heavy(1)
        reciprocal(2)
        reciprocal(3)
        for t in (1, 0):
            fetch_recip(t, all_queries)
        for cols in query_half:
            for t in (2, 3):
                fetch_recip(t, cols)
        match_plain(3)
        pair_sum(2)
        pair_sum(3)
        group_sum(2)
        group_sum(3)
        hidden(1, all_queries)
        hidden(0, all_queries)
        for h, cols in enumerate(query_half):
            size_times_sel(3, cols)
            size_times_sel(2, cols)
            hidden(3, cols)
            hidden(2, cols)
            interleave(h)

        blocks = N // P
        for h, cols in enumerate(query_half):
            codes = keep.tile([P, HALF_U], U32, name="codes%d" % h, align_bytes=64)
            hid_scales = keep.tile([P, HALF_U], U8, name="hid_scales%d" % h, align_bytes=64)
            nc.vector.quantize_mx(
                out=codes[:].bitcast(FP8X4), scales=hid_scales[:], in_=grouped[h][:].rearrange("p r t -> p (r t)"))
            for m in range(blocks):
                acc = psum.tile([P, BANK], F32, name="acc", tag="bank%d" % (blocks * h + m))
                nc.tensor.matmul_mx(
                    out=acc[:, 0:HALF_U],
                    lhsT=w3_words_sb[:, 2 * P * m:2 * P * (m + 1)].bitcast(FP4X4),
                    lhsT_scale=w3_scales_sb[:, P * m:P * (m + 1)],
                    rhs=codes[:].bitcast(FP8X4), rhs_scale=hid_scales[:], start=True, stop=True)
                result = keep.tile([P, HALF_U], F32, name="result%d_%d" % (h, m))
                copy = nc.vector.tensor_copy if (h, m) == (1, blocks - 1) else nc.scalar.copy
                copy(result[:], acc[:, 0:HALF_U])
                nc.sync.dma_start(out[P * m:P * (m + 1), cols], result[:])
